import numpy as np, ml_dtypes
CORES = [3,11,19,27,35,43,51,59]
N = 8
BF = ml_dtypes.bfloat16
def gentries(a):
    return np.ascontiguousarray(a.reshape(8, 16, -1).transpose(0, 2, 1)).reshape(8, -1)
def gtable(e):
    e = np.asarray(e); return np.ascontiguousarray(e.reshape(8, -1, 16).transpose(0, 2, 1)).reshape(128, -1).astype(np.int32)
V, C, H, NCL, ST, Q = 2048, 128, 2048, 16, 3, 48
LANE = np.arange(16)
def look(xs, l):
    a = np.take_along_axis(xs, l[:, None, :], 2).reshape(8, 16, C, 16)
    return a, np.max(a, axis=3) - np.min(a, axis=3)
def best(s, w, tag):
    u = np.add.reduce(w[:, :, :, None] * s[:, :, None, :], axis=1) & (H - 1)
    u1, u2 = u[:, 0], u[:, 1]
    h = (((u1 * u2) >> 5)[:, None, :] + (2 * LANE[:, None] + 1) * u2[:, None, :]) & (H - 1)
    cost = np.stack([np.add.reduce(np.abs(np.take_along_axis(tag, h[:, m:m + 1], 2) - s), axis=1) for m in range(16)], axis=1)
    m = np.argmin(cost, axis=1)
    return h, np.min(cost, axis=1), np.take_along_axis(h, m[:, None, :], 1)[:, 0]
def start(x, l, w, tag):
    o = []
    for r in range(N):
        s = look(x[r], l[r, :, r % NCL])[1]; h, least, hs = best(s, w[r], tag[r]); o.append((s, h, least))
    return [np.stack(z) for z in zip(*o)]
def mid(rng, least):
    return np.take_along_axis(np.sort(least, axis=-1), rng.integers(C // 5, 4 * C // 5, (N, 8, 1)), -1)[..., 0]
def parts(rng):
    x = rng.integers(0, 256, (N, 8, 16, V)); l = np.argsort(rng.random((N, 8, NCL, V)), axis=-1)
    tag = np.minimum((256 * rng.beta(15.0, 2.0, (N, 8, 16, H))).astype(np.int64), 255)
    e = np.argsort(rng.random((N, 8, H, 16)), axis=-1); f = np.argsort(e, axis=-1)
    return x, l, tag, np.ascontiguousarray((e + 16 * f).transpose(0, 1, 3, 2)), rng.integers(1, 256, (N, 8, 16, 2))
def plant(rng, s, h, tag, ids, n, dev, used, copies=1):
    done = []
    for i in ids:
        if len(done) == n: break
        i = int(i); free = sorted(set(int(z) for z in h[:, i]) - used)
        if len(free) < copies: continue
        for j in rng.permutation(len(free))[:copies]:
            z = free[int(j)]; used.add(z); p = int(rng.integers(0, 16)); tag[:, z] = s[:, i]
            tag[p, z] = s[p, i] + (dev if s[p, i] < 128 else -dev)
        done.append(i)
    return done
def wear(rng, x, ix, s):
    lo = (rng.random(s.shape) * (256 - s)).astype(np.int64); k = rng.integers(0, 16, s.shape); k2 = (k + rng.integers(1, 16, s.shape)) & 15
    a = lo[..., None] + (rng.random(s.shape + (16,)) * (s[..., None] + 1)).astype(np.int64)
    np.put_along_axis(a, k[..., None], lo[..., None], 2); np.put_along_axis(a, k2[..., None], (lo + s)[..., None], 2)
    x[:, ix] = a.reshape(16, -1)
def still(rng, x, ix, tag):
    s = rng.integers(20, 181, (16, C)); s[:2] = 0; z = np.zeros(C, np.int64)
    o = rng.permutation(C); a = np.sort(o[:Q + 3]); b = o[Q + 3:]
    z[a] = H // 2 + 2 + 2 * rng.permutation(H // 4 - 1)[:Q + 3]; z[b] = 1 + 2 * rng.permutation(H // 2 - 1)[:C - Q - 3]
    z[b[0]] = H - 1
    z[a[Q - 1]] = z[a[0]]; z[a[Q - 3]] = z[a[1]]; z[a[Q - 2]] = z[a[1]]
    s[2] = z >> 4; s[3] = z & 15
    v = s[4:, a[0]]; s[4:, a[Q - 1]] = np.where(v < 100, v + 100, v - 100)
    s[4:, a[Q - 3]] = s[4:, a[1]] - 3; s[4:, a[Q - 2]] = s[4:, a[1]] + 3
    s[:, a[2]] = 0; s[:, b[1]] = np.where(LANE < 4, 0, 3); tag[:, 0] = np.where(LANE < 4, 0, 6)
    c = np.concatenate([b[:1], b[10:]]); tag[:, z[c]] = s[:, c]
    for j in range(8):
        i = int(b[2 + j]); s[:4, i] = np.array([255, 9, 255, 7] if j < 4 else [255, 7, 255, 9])
        u1 = (4080 + int(s[1, i])) & (H - 1); u2 = (4080 + int(s[3, i])) & (H - 1)
        tag[:, (((u1 * u2) >> 5) + (8 * (j & 3) + 1) * u2) & (H - 1)] = s[:, i]
    wear(rng, x, ix, s)
def pack(x, l, tag, ef, w, th):
    b = lambda a, n: np.ascontiguousarray(a).reshape(N, 128, n).astype(np.float32).astype(BF)
    return {"x": b(x, V), "nb": np.stack([gtable(a.reshape(8, -1)) for a in l]), "tag": b(tag, H), "ef": b(ef, H), "w": b(w, 2),
            "th": np.ascontiguousarray(np.repeat(th, 16, axis=1)[:, :, None]).astype(np.int32)}
def setup_inputs(rng):
    x, l, tag, ef, w = parts(rng); s, h, least = start(x, l, w, tag)
    return pack(x, l, tag, ef, w, mid(rng, least))
def setup_inputs_room(rng):
    x, l, tag, ef, w = parts(rng); s, h, least = start(x, l, w, tag); th = np.zeros((N, 8), np.int64)
    for r in range(N):
        for g in range(8):
            n = int(rng.choice(np.array([0, 1, Q - 1, Q, Q + 1, C]))); t = int(rng.choice(np.array([0, 1, 20])))
            if r == 0: n = (Q, Q + 1, Q - 1, 0, 1, C, Q, Q + 1)[g]
            if n == 0:
                th[r, g] = 4080; continue
            used = set(); ids = rng.permutation(C); done = set(plant(rng, s[r, g], h[r, g], tag[r, g], ids, C - n, t, used))
            plant(rng, s[r, g], h[r, g], tag[r, g], [i for i in ids if int(i) not in done], n // 2, t + 1, used); th[r, g] = t
    return pack(x, l, tag, ef, w, th)
def setup_inputs_ties(rng):
    x, l, tag, ef, w = parts(rng); s, h, least = start(x, l, w, tag); th = np.zeros((N, 8), np.int64)
    for r in range(N):
        for g in range(8):
            th[r, g] = int(rng.choice(np.array([0, 1, 20])))
            plant(rng, s[r, g], h[r, g], tag[r, g], rng.permutation(C), C // 2, int(th[r, g]), set(), 2)
    for g in (3, 5): tag[:, g] = tag[:, g, :, :1].copy()
    t = mid(rng, start(x, l, w, tag)[2])
    for g in (3, 5): th[:, g] = t[:, g]
    return pack(x, l, tag, ef, w, th)
def setup_inputs_hash(rng):
    x, l, tag, ef, w = parts(rng)
    w[:, 0, :, 1] = 0; w[:, 1, :, 0] = 0; w[:, 2] = 0; w[:, 2, 5] = np.array([3, 255]); w[:, 3] = 255; w[:, 4, :, 1] = 128
    x[:, 5] = 255 * rng.integers(0, 2, (N, 16, V)); x[:, 6] = rng.integers(0, 256, (N, 16, 1))
    tag[0, 5] = rng.integers(0, 5, (16, H)); tag[1, 5] = 0
    w[:, 7] = 0; w[:, 7, :4] = np.array([[16, 0], [1, 0], [0, 16], [0, 1]]); l[:, 7] = l[:, 7, :1].copy()
    for r in range(N): still(rng, x[r, 7], l[r, 7, 0], tag[r, 7])
    th = mid(rng, start(x, l, w, tag)[2]); th[::2, 5] = np.maximum(th[::2, 5] - 1, 0); th[1::2, 0] = 4080; th[:, 7] = 40
    return pack(x, l, tag, ef, w, th)
def setup_inputs_ends(rng):
    x, l, tag, ef, w = parts(rng)
    l[:, 0] = np.arange(V); l[:, 1] = np.arange(V)[::-1]; l[:, 2] = l[:, 2, :1].copy()
    ef[:, 4] = (17 * LANE)[:, None]; ef[:, 5] = (17 * (15 - LANE))[:, None]; ef[:, 6] = (((LANE + 1) & 15) + 16 * ((LANE + 15) & 15))[:, None]
    q = rng.permutation(N); x[q[2:4]] = rng.integers(0, 8, (2, 8, 16, V)); tag[q[2:4]] = rng.integers(240, 256, (2, 8, 16, H))
    th = mid(rng, start(x, l, w, tag)[2]); th[q[0]] = 0; th[q[1]] = 4080
    return pack(x, l, tag, ef, w, th)
def setup_inputs_spread(rng):
    x, l, tag, ef, w = parts(rng)
    x = (np.exp2(8 * rng.random((N, 8, 1, V))) * rng.random((N, 8, 16, V))).astype(np.int64)
    tag = (np.exp2(8 * rng.random((N, 8, 1, H))) * rng.random((N, 8, 16, H))).astype(np.int64)
    x = np.minimum(x, 255); tag = np.minimum(tag, 255)
    w = np.minimum(np.exp2(8 * rng.random((N, 8, 16, 2))).astype(np.int64), 255)
    return pack(x, l, tag, ef, w, mid(rng, start(x, l, w, tag)[2]))
def check_inputs(d):
    bad = []
    for k, hi in (("x", 255), ("nb", V - 1), ("tag", 255), ("ef", 255), ("w", 255), ("th", 4080)):
        v = np.asarray(d[k]).astype(np.float32)
        if not (np.all(v >= 0) and np.all(v <= hi) and np.all(v == np.floor(v))): bad.append("range of " + k)
    if bad: return bad
    l = np.stack([gentries(a) for a in d["nb"]]).reshape(N, 8, NCL, V)
    if np.any(np.sort(l, axis=-1) != np.arange(V)): bad.append("sites of a class all different")
    b = np.asarray(d["ef"]).astype(np.float32).astype(np.int64).reshape(N, 8, 16, H); e = b & 15; f = b >> 4
    if np.any(np.sort(e, axis=2) != LANE[:, None]) or np.any(np.take_along_axis(f, e, 2) != LANE[:, None]): bad.append("e a permutation, f its inverse")
    t = np.asarray(d["th"]).reshape(N, 8, 16)
    if np.any(t != t[:, :, :1]): bad.append("th alike in a group")
    return bad
def reference(x, nb, tag, ef, w, th):
    whole = lambda a, n: a.astype(np.float32).astype(np.int64).reshape(N, 8, 16, n)
    xs, tg, pf, ws = whole(x, V), whole(tag, H), whole(ef, H), whole(w, 2)
    lim = th.astype(np.int64).reshape(N, 8, 16)[:, :, :1]
    l = np.stack([gentries(a) for a in nb]).astype(np.int64).reshape(N, 8, NCL, V)
    cl = [r % NCL for r in range(N)]
    for t in range(ST):
        sig, home, miss = [], [], []
        for r in range(N):
            ix = l[r, :, cl[r]]; a, s = look(xs[r], ix)
            h, least, hs = best(s, ws[r], tg[r]); hit = least <= lim[r]
            f = np.take_along_axis(pf[r] >> 4, hs[:, None, :], 2)
            f = np.where(hit[:, None, :], f, LANE[:, None])
            a = np.take_along_axis(a, f.transpose(0, 2, 1)[:, None, :, :], 3).reshape(8, 16, V)
            for g in range(8): xs[r, g][:, ix[g]] = a[g]
            sig.append(s); home.append(h[:, 0]); miss.append(~hit); cl[r] = int(np.sum(least)) & (NCL - 1)
        new = []
        for r in range(N):
            q = (r + 1 + t % (N - 1)) % N
            far = best(sig[r], ws[q], tg[q])[2]; back = np.take_along_axis(pf[q], far[:, None, :], 2)
            for g in range(8):
                i = np.flatnonzero(miss[r][g])[:Q]
                col, first = np.unique(home[r][g, i], return_index=True); i = i[first]
                new.append((r, g, col, sig[r][g][:, i], back[g][:, i]))
        for r, g, col, s, b in new:
            tg[r, g][:, col] = s; pf[r, g][:, col] = (b >> 4) + 16 * (b & 15)
    return {"y": xs.reshape(N, 128, V).astype(np.float32).astype(BF)}

@@ -1,0 +1,518 @@
+from concourse.mybir import AluOpType, AxisListType, ActivationFunctionType
+
+F, B, I, U, H = "float32", "bfloat16", "int32", "uint16", "float16"
+SCRATCH = {}
+for _n in ("X", "A", "A2", "MX", "MN", "E", "D", "R"):
+    SCRATCH[_n] = ("sbuf", [128, 2048], B)
+for _n, _w, _d in (
+        ("SG", 144, B), ("SN", 128, B), ("IB", 128, B), ("IBN", 128, B),
+        ("TG", 2112, B), ("EF", 2112, B), ("NB", 2048, I), ("NB0", 128, I), ("IO", 2048, F), ("W32", 2048, F),
+        ("IVF", 128, F), ("IV", 128, U), ("NBU", 128, U), ("PHI", 128, I), ("PHA", 128, I), ("PHU", 128, U),
+        ("WW", 8, B), ("TH", 8, I), ("PI", 8, I), ("CI", 8, I), ("CF", 16, F), ("JG", 128, F),
+        ("J", 240, F), ("LMP", 240, H), ("LMN", 240, H),
+        ("RST", 512, B), ("BIG", 512, B), ("W1", 128, B), ("W2", 128, B), ("W1N", 128, B), ("W2N", 128, B), ("B1", 8, B),
+        ("TH8", 8, F), ("ONE", 264, F), ("ONB", 264, B), ("SPR", 264, B), ("C1", 264, F), ("C2", 264, F),
+        ("KS", 264, F), ("EQ", 264, F), ("HS", 264, F), ("Z3", 264, H), ("KS2", 264, F), ("EQ2", 264, F), ("HS2", 264, F), ("Z32", 264, H),
+        ("BASE", 128, F), ("I8", 8, F), ("I8S", 8, F), ("RS", 384, B), ("P0", 128, B), ("SEL", 144, B),
+        ("MASK", 144, B), ("CAP", 152, F), ("VAL", 152, F), ("YS", 152, F),
+        ("UI", 256, I), ("UA", 256, I), ("U1", 128, F), ("PP", 128, I), ("HI", 136, I), ("HU", 128, U), ("HF", 128, H),
+        ("HI2", 48, I), ("UI2", 96, I), ("UA2", 96, I), ("U12", 48, F), ("PP2", 48, I), ("HU2", 48, U), ("SN2", 128, B),
+        ("OE", 8, U), ("OF", 8, U), ("VE", 128, F), ("OS", 128, U), ("OE2", 8, U),
+        ("CC", 8, F), ("RC", 8, F), ("QI", 8, I), ("NC", 8, F), ("OC", 8, U),
+        ("FL", 128, B), ("CN", 128, B), ("LE", 384, B), ("LS", 384, B), ("L1", 8, U), ("HC", 48, H),
+        ("OW0", 8, U), ("OW1", 8, U), ("SC0", 48, B), ("SC1", 48, B), ("RQ0", 48, B), ("RQ1", 48, B),
+        ("RI", 48, I), ("AN0", 48, I), ("AN1", 48, I), ("RB0", 48, I), ("RB1", 48, I)):
+    SCRATCH[_n] = ("sbuf", [128, _w], _d)
+for _n in ("PU", "PK", "PK2", "PH", "PO", "PM", "PD0", "PD1"):
+    SCRATCH[_n] = ("psum", [128, 512], F)
+
+SEMAPHORES = ["cg", "cv", "cs", "ct", "rq0", "rq1", "rb0", "rb1", "sq0", "sq1", "sb0", "sb1"] + ["d%d" % _i for _i in range(24)]
+
+ST, NQ = 3, 48
+MAGIC = 12582912.0
+CFG = {"cyc": 1.04e-3, "fix": 0.06, "wake": 0.3, "gather": 1.7, "scatter": 3.8, "pe": 0.52e-3, "dma": 2.0, "bw": 250e3,
+       "remote": 4, "first": 3, "table": 1.3, "inv": "vs", "seed": 70299, "noise": 0.2, "piece": 2, "out": [2, 4, 6, 8],
+       "spare": 0.4, "rounds": 8, "tp": 16, "tags": ["s", "v", "vs", "v"], "far": ["vs", "vs"],
+       "tweaks": [(0, 0.3), (35, -3), (36, -3), (37, -3), (38, -3), (49, -1), (86, -3), (87, -3), (88, -3), (89, -3), (139, 3),
+                  (175, -3), (176, -3), (177, -3), (178, -3), (307, 3), (308, 2), (309, -1), (310, -1), (311, -1), (373, -3),
+                  (374, -3), (375, -3), (376, -3), (391, -1), (392, -1)],
+       "force": {81: "s", 356: "v", 102: "s"}}
+
+
+def schedule(ops):
+    n, wake = len(ops), CFG["wake"]
+    pred = [set() for _ in ops]
+    wrote, readers, bank = {}, {}, {}
+    for k, o in enumerate(ops):
+        for r in o["R"] + o["after"]:
+            if r in wrote:
+                pred[k].add(wrote[r])
+        for w in o["W"]:
+            if w in wrote:
+                pred[k].add(wrote[w])
+            pred[k].update(readers.get(w, []))
+        for b in o["P"]:
+            if b in bank:
+                pred[k].add(bank[b])
+            bank[b] = k
+        for r in o["R"]:
+            readers.setdefault(r, []).append(k)
+        for w in o["W"] + o["marks"]:
+            wrote[w] = k
+            readers[w] = []
+        pred[k].discard(k)
+    succ = [[] for _ in ops]
+    for k in range(n):
+        for p in pred[k]:
+            succ[p].append(k)
+
+    def gap(p, y):
+        return ops[p]["late"] + (0.0 if ops[p]["qs"] == ops[y]["qs"] == "t" else wake)
+
+    def sweep(prio, back, force=None):
+        before, behind = (succ, pred) if back else (pred, succ)
+        left = [len(b) for b in before]
+        ready = [k for k in range(n) if not left[k]]
+        taken = {q: [] for q in "gvsty"}
+        start, where = [0.0] * n, [""] * n
+        while ready:
+            k = min(ready, key=lambda j: (prio[j], j))
+            ready.remove(k)
+            can = ops[k]["late"] if back else 0.0
+            for p in before[k]:
+                can = max(can, start[p] + ops[p]["busy"] + (gap(k, p) if back else gap(p, k)))
+            best = None
+            for q in (force or {}).get(k, ops[k]["qs"]):
+                s, at = can, 0
+                for a, b in taken[q]:
+                    if s + ops[k]["busy"] <= a + 1e-9:
+                        break
+                    s = max(s, b)
+                    at += 1
+                s_cmp = s + (CFG["spare"] if q == "v" else 0.0)
+                if best is None or s_cmp < best[0]:
+                    best = (s_cmp, s, q, at)
+            _, s, q, at = best
+            taken[q].insert(at, (s, s + ops[k]["busy"]))
+            start[k], where[k] = s, q
+            for y in behind[k]:
+                left[y] -= 1
+                if not left[y]:
+                    ready.append(y)
+        end = max(start[k] + ops[k]["busy"] + (0.0 if back else ops[k]["late"]) for k in range(n))
+        return start, where, end
+
+    x = 12345 + 977 * CFG["seed"]
+    prio = [0.0] * n
+    for k in reversed(range(n)):
+        x = (x * 1103515245 + 12345) % 2147483648
+        prio[k] = min([prio[y] - gap(k, y) for y in succ[k]] + [-ops[k]["late"]]) - ops[k]["busy"] - CFG["noise"] * x / 2147483648
+    best = None
+    for _ in range(CFG["rounds"]):
+        start, where, end = sweep(prio, False)
+        if best is None or end < best[2]:
+            best = (start, where, end)
+        late, _w, _e = sweep([-(start[k] + ops[k]["busy"]) for k in range(n)], True)
+        prio = [-(late[k] + ops[k]["busy"]) for k in range(n)]
+    prio = list(best[0])
+    for k, d in CFG["tweaks"]:
+        prio[k] += d
+    start, where, end = sweep(prio, False, CFG["force"])
+    return [(k, where[k]) for k in sorted(range(n), key=lambda j: (start[j], j))]
+
+
+def rank_program(g, core, T, topo):
+    rank = T.rank_of(core)
+    if rank is None:
+        return
+    N = len(T.cores)
+    Op, Act = AluOpType, ActivationFunctionType
+    add, sub, mul, mx, mn = Op.add, Op.subtract, Op.mult, Op.max, Op.min
+    Q = {"g": g, "v": g.vector, "s": g.scalar, "t": g.tensor, "y": g.sync}
+    V, S, PE = g.vector, g.scalar, g.tensor
+    ops = []
+
+    def record(kind, qs, fn, R, W, P, busy, late=0.0, after=(), marks=(), sem=None):
+        ops.append(dict(kind=kind, qs=qs, fn=fn, R=list(R), W=list(W), P=list(P), busy=busy, late=late, after=list(after),
+                        marks=list(marks), sem=sem))
+
+    def cyc(n):
+        return max(n, 64) * CFG["cyc"] + CFG["fix"]
+
+    def op(qs, fn, n, R, W, P=(), table=False):
+        after = ["sent." + r for r in R if r[:2] in ("RQ", "RB")]
+        record("c", qs, lambda q: [fn(q)], R, W, P, cyc(n) + (CFG["table"] if table else 0.0), after=after)
+
+    def dma(q, out, in_, nbytes, R, W, more=0.0):
+        record("d", q, lambda q: Q[q].dma_start(out, in_), R, W, (), 0.1, CFG["dma"] + nbytes / CFG["bw"] + more)
+
+    sent = [0]
+
+    def send(dst_rank, name, src, rsem, lsem):
+        dst = T.cores[dst_rank]
+        rid, pid, _ = topo.addr(dst)
+        record("r", "g", lambda q: g.remote_dma(T[name][:], T[src][:], T.sem[rsem], T.sem[lsem], pid, rid, topo.mask(core, dst)),
+               [src], [], (), 0.5, CFG["remote"] + (0.0 if sent[0] else CFG["first"]), marks=["sent." + name],
+               sem=(lsem, len(topo.engines(core, dst))))
+        sent[0] = 1
+
+    def ts(n, out, in0, s1, s2, o0, o1, R, W, P=()):
+        if o1 is None:
+            op("v", lambda q: V.tensor_scalar(out, in0, s1, None, o0), n, R, W, P)
+        else:
+            op("v", lambda q: V.tensor_scalar(out, in0, s1, s2, o0, o1), n, R, W, P)
+
+    def tt(n, out, a, b, o, R, W, P=()):
+        op("v", lambda q: V.tensor_tensor(out, a, b, o), n, R, W, P)
+
+    def cp(n, out, in_, R, W, P=()):
+        op("v", lambda q: V.tensor_copy(out, in_), n, R, W, P)
+
+    def scan(n, out, d0, d1, o0, o1, R, W, P=()):
+        op("v", lambda q: V.tensor_tensor_scan(out, d0, d1, 0.0, o0, o1), n, R, W, P)
+
+    def fill(n, ap, c, W, P=()):
+        op("v", lambda q: V.memset(ap, c), n, [], W, P)
+
+    def mms(n, items, R, bk):
+        after = ["sent." + r for r in R if r[:2] == "RQ"]
+        record("c", "t", lambda q: [PE.matmul(*it) for it in items], R, [], [bk], n * CFG["pe"], after=after)
+
+    def gp(fn, n, R, W):
+        record("c", "g", lambda q: [fn()], R, W, (), 0.17 + 2 * n * CFG["cyc"])
+
+    def iota(n, out, pat, base, cm, W, flt=True):
+        if flt:
+            gp(lambda: g.iota(out, pat, base, cm, allow_small_or_imprecise_dtypes=True), n, [], W)
+        else:
+            gp(lambda: g.iota(out, pat, base, cm), n, [], W)
+
+    def asel(n, out, in_, pat, cmp, base, cm, R, W, other=0.0):
+        gp(lambda: g.affine_select(out, in_, pat, cmp, other, base, cm), n, R, W)
+
+    def gfill(out, n, c, W):
+        asel(n, out, T.ONE[:, 0:n], [[0, n]], Op.is_equal, 1, 0, ["ONE"], W, c)
+
+    def parts(name, n=8):
+        return ["%s.%d" % (name, k) for k in range(n)]
+
+    GA, SC = CFG["gather"], CFG["scatter"]
+
+    def copy(q, out, in_):
+        return V.tensor_copy(out, in_) if q == "v" else S.activation(out, in_, Act.Copy)
+
+    def pick(n, out, win, R, W, qs="vs"):
+        op(qs, lambda q: copy(q, out, win), n * GA, R, W)
+
+    def gather(dst, src, off, k0=0, k1=8):
+        w = CFG["piece"]
+        for k in range(k0, k1, w):
+            pick(256 * w, T[dst][:, 256 * k:256 * (k + w)], T[src][:, 0:2048].indirect(T[off][:, 16 * k:16 * (k + w)]),
+                 parts(src) + [off], parts(dst)[k:k + w])
+
+    cR, cG, cM, cT, cW1, cW2, cN1, cN2 = [T.CF[:, k:k + 1] for k in range(8)]
+    cL = T.CF[:, 12:13]
+
+    c0 = rank % 16
+    dma("s", T.NB0[:], T.nb[:, 128 * c0:128 * c0 + 128], 65536, [], ["NB0"])
+    dma("y", T.X[:], T.x[:], 524288, [], parts("X"))
+    dma("s", T.WW[:, 0:2], T.w[:], 0, [], ["WW"])
+    dma("y", T.TG[:, 0:2048], T.tag[:], 524288, ["X.0"], ["TGa"])
+    dma("y", T.TH[:, 0:1], T.th[:], 0, ["X.0"], ["TH"])
+    dma("y", T.EF[:, 0:2048], T.ef[:], 524288, ["X.0"], ["EFa"], 2.0)
+    dma("y", T.NB[:], T.nb[:], 1048576, ["TGa"], ["NB"])
+    TG, EF = ["TGa", "TGb"], ["EFa", "EFb"]
+
+    fill(1024, T.E[:], 1.0, ["E"])
+    fill(132, T.ONB[:], 1.0, ["ONB"])
+    iota(1, T.PI[:, 0:1], [[0, 1]], 0, 1, ["PI"], False)
+    iota(128, T.JG[:], [[1, 8], [0, 16]], 0, 0, ["JG"])
+    iota(512, T.IO[:, 0:512], [[1, 512]], 64, 0, ["IO.0"])
+    asel(128, T.IB[:], T.ONB[:, 0:128], [[-1, 128]], Op.is_equal, 0, 1, ["ONB"], ["IB"])
+    asel(2048, T.E[:], T.E[:], [[-1, 128], [0, 16]], Op.is_equal, 0, 1, ["E"], ["E"])
+    iota(264, T.ONE[:], [[0, 264]], 1, 0, ["ONE"])
+    asel(264, T.SPR[:], T.ONB[:], [[-16, 8], [-1, 33]], Op.is_equal, 0, 1, ["ONB"], ["SPR"])
+    asel(264, T.SPR[:], T.SPR[:], [[0, 8], [-1, 33]], Op.is_ge, 15, 0, ["SPR"], ["SPR"])
+    gfill(T.C1[:], 264, -1.0 / 16, ["C1"])
+    gfill(T.C1[:, 0::33], 8, 1.0e6, ["C1"])
+    gfill(T.C1[:, 16::33], 8, 15.0 / 32, ["C1"])
+    gfill(T.C1[:, 17::33], 8, 15.0 / 32, ["C1"])
+    asel(264, T.C2[:], T.ONE[:], [[0, 8], [-16, 33]], Op.is_ge, 256, 1, ["ONE"], ["C2"])
+    iota(8, T.C2[:, 0::33], [[0, 8]], 0, 0, ["C2"])
+    iota(24, T.HS[:, 240:264], [[0, 24]], 0, 0, ["HS"])
+    iota(24, T.HS2[:, 240:264], [[0, 24]], 0, 0, ["HS2"])
+    iota(240, T.J[:], [[1, 240]], 0, 0, ["J"])
+    iota(128, T.BASE[:], [[256, 128]], 0, 0, ["BASE"])
+    iota(384, T.RS[:], [[0, 384]], 1, 0, ["RS"])
+    iota(3, T.RS[:, 0::128], [[0, 3]], 0, 0, ["RS"])
+    iota(16, T.SG[:, 128:144], [[0, 16]], 0, 0, ["SGb"])
+    iota(8, T.HI[:, 128:136], [[0, 8]], 6144, 0, ["HIb"], False)
+    asel(128, T.P0[:], T.ONB[:, 0:128], [[-16, 8], [0, 16]], Op.is_equal, 0, 1, ["ONB"], ["P0"])
+    iota(144, T.SEL[:], [[0, 144]], 0, 0, ["SEL"])
+    asel(8, T.SEL[:, 15:143:16], T.ONB[:, 0:8], [[-16, 8]], Op.is_equal, 0, 1, ["ONB"], ["SEL"])
+    iota(3, T.VAL[:, 0:147:49], [[0, 3]], 0, 0, ["VALz"])
+
+    def positions(c):
+        op("s", lambda q: S.activation(T.IO[:, 512 * c:512 * c + 512], T.IO[:, 0:512], Act.Identity, 512.0 * c), 512,
+           ["IO.0"], ["IO.%d" % c])
+    for c in range(1, 4):
+        positions(c)
+
+    fill(256, T.RST[:], 1.0, ["RST"])
+    fill(256, T.BIG[:], 0.0, ["BIG"])
+    ts(1, T.CI[:, 0:1], T.PI[:, 0:1], 15, None, Op.bitwise_and, None, ["PI"], ["CI0"])
+    ts(1, T.CI[:, 1:2], T.PI[:, 0:1], 4, None, Op.arith_shift_right, None, ["PI"], ["CI1"])
+    fill(1, T.RST[:, 0::16], 0.0, ["RST"])
+    fill(1, T.BIG[:, 0::16], 256.0, ["BIG"])
+    cp(1, T.CF[:, 0:2], T.CI[:, 0:2], ["CI0", "CI1"], ["cR"])
+    fill(1, T.TG[:, 2048:2112], 0.0, ["TGb"])
+    fill(1, T.EF[:, 2048:2112], 0.0, ["EFb"])
+    ts(1, cM, cR, 64.0, 32.0, mul, add, ["cR"], ["cM"])
+    ts(1, T.B1[:], T.JG[:, 0::16], cG, None, Op.is_equal, None, ["JG", "cR"], ["B1"])
+    cp(1, T.CF[:, 4:6], T.WW[:, 0:2], ["WW"], ["cW"])
+    ts(1, T.CF[:, 6:8], T.WW[:, 0:2], -1.0, None, mul, None, ["WW"], ["cN"])
+    for nm, col in (("W1", cW1), ("W2", cW2), ("W1N", cN1), ("W2N", cN2)):
+        ts(128, T[nm][:], T.JG[:], cG, col, Op.is_equal, mul, ["JG", "cR", "cW", "cN"], [nm])
+    ts(1, T.IBN[:], T.IB[:], -1.0, None, mul, None, ["IB"], ["IBN"])
+    fill(264, T.PK[:, 0:264], 1.0e6, [], ["PK"])
+    fill(264, T.PK2[:, 0:264], 1.0e6, [], ["PK2"])
+    ts(1, cT, T.TH[:, 0:1], 31.0 / 32, 1.0 / 16, add, mul, ["TH"], ["cT"])
+    ts(1, cL, cR, 112.0, None, add, None, ["cR"], ["cL"])
+    ts(1, T.TH8[:], T.JG[:, 0::16], cG, cT, Op.is_equal, mul, ["JG", "cR", "cT"], ["TH8"])
+    ts(240, T.LMP[:], T.J[:], cL, None, Op.is_equal, None, ["J", "cL"], ["LMP"])
+    ts(120, T.LMN[:], T.LMP[:], -1.0, None, mul, None, ["LMP"], ["LMN"])
+    ts(1, T.EF[:, 2048:2049], cR, 17.0, None, mul, None, ["cR"], ["EFb"])
+    ts(1, T.I8[:], T.JG[:, 0::16], 16.0, cR, mul, add, ["JG", "cR"], ["I8"])
+    for a in range(3):
+        ts(1, T.MASK[:, 48 * a:48 * a + 48], T.J[:, 0:48], T.I8[:, a:a + 1], 2.0, Op.is_ge, mul, ["J", "I8"], ["MASK%d" % a])
+    ts(1, T.I8S[:], T.I8[:], 1.0 / 128, None, mul, None, ["I8"], ["I8S"])
+    ts(1, T.CF[:, 8:11], T.I8[:, 0:3], 16.0, 1.0 / 4096, add, mul, ["I8"], ["cC"])
+    for a in range(3):
+        ts(1, T.CAP[:, 49 * a:49 * a + 49], T.J[:, 0:49], 0.0, T.CF[:, 8 + a:9 + a], mul, add, ["J", "cC"], ["CAP%d" % a])
+    fill(1, T.CAP[:, 0:147:49], -1.0, ["CAP0", "CAP1", "CAP2"])
+
+    def class_lists(n, src, R):
+        cp(n, T.NBU[:], src, R, ["NBU"])
+        ts(128, T.PHI[:], T.NBU[:], 128.0625, -15.0 / 32, mul, add, ["NBU"], ["PHI"])
+        ts(128, T.PHA[:], T.PHI[:], 2047, None, Op.bitwise_and, None, ["PHI"], ["PHA"])
+        cp(128, T.PHU[:], T.PHA[:], ["PHA"], ["PHU"])
+
+    def invert_piece(k, first):
+        win = T.W32[:, 0:2048].indirect(T.PHU[:, 16 * k:16 * k + 16])
+        src = T.IO[:, 256 * k:256 * k + 256]
+        op(CFG["inv"], lambda q: V.tensor_copy(win, src) if q == "v" else S.activation(win, src, Act.Silu), 256 * SC,
+           ["PHU", "IO.%d" % (k // 2)], ["W32"], table=first)
+
+    def invert(t):
+        for k in range(8):
+            invert_piece(k, t == 0 and k == 0)
+        dma("y", T.IVF[:], T.W32[0:128:16, :], 65536, ["W32"], ["IVF"])
+        ts(128, T.IV[:], T.IVF[:], -64.0, None, add, None, ["IVF"], ["IV"])
+
+    def sites_in_class_order():
+        gather("A", "X", "NBU")
+        for c in range(4):
+            a = T.A[:, 512 * c:512 * c + 512]
+            R = parts("A")[2 * c:2 * c + 2]
+            scan(256, T.MX[:, 512 * c:512 * c + 512], T.RST[:], a, mul, mx, R + ["RST"], ["MX.%d" % c])
+            scan(256, T.MN[:, 512 * c:512 * c + 512], T.BIG[:], a, add, mn, R + ["BIG"], ["MN.%d" % c])
+
+    def hashes(n, plus, minus, R, x):
+        items = []
+        for k, (wp, wn) in enumerate((("W1", "W1N"), ("W2", "W2N"))):
+            out = T.PU[:, k * n:k * n + n]
+            items.append((out, T[wp][:], plus, True, minus is None))
+            if minus is not None:
+                items.append((out, T[wn][:], minus, False, True))
+        items.append((T.PU[0:n, 256:384], plus, T.IBN[:], True, minus is None))
+        if minus is not None:
+            items.append((T.PU[0:n, 256:384], minus, T.IB[:], False, True))
+        mms(128 * len(items), items, R + ["W1", "W2", "W1N", "W2N", "IB", "IBN"], "PU")
+        UI, UA, U1, PP, HI, HU, SN = [nm + x for nm in ("UI", "UA", "U1", "PP", "HI", "HU", "SN")]
+        cp(2 * n, T[UI][:, 0:2 * n], T.PU[:, 0:2 * n], [], [UI], ["PU"])
+        op("vs", lambda q: copy(q, T[SN][0:n, :], T.PU[0:n, 256:384]), 128, [], [SN], ["PU"])
+        ts(2 * n, T[UA][:, 0:2 * n], T[UI][:, 0:2 * n], 2047, None, Op.bitwise_and, None, [UI], [UA])
+        ts(n, T[U1][:, 0:n], T[UA][:, 0:n], cM, None, add, None, [UA, "cM"], [U1])
+        tt(2 * n, T[PP][:, 0:n], T[U1][:, 0:n], T[UA][:, n:2 * n], mul, [U1, UA], [PP])
+        ts(n, T[HI][:, 0:n], T[PP][:, 0:n], 5, 2047, Op.arith_shift_right, Op.bitwise_and, [PP], [HI])
+        cp(n, T[HU][:, 0:n], T[HI][:, 0:n], [HI], [HU])
+
+    def events_by_centre(n, HI):
+        ts(n, T.HF[:, 0:n], T[HI][:, 0:n], -2048.0, 1.0 / 4096, add, mul, [HI], ["HF"])
+        mms(264, [(T.PH[0:n, 0:264], T.HF[:, 0:n], T.SPR[:], True, True)], ["HF", "SPR"], "PH")
+
+    def distances(n, lo, hi, bk, x, qs):
+        w = 16 * (hi - lo)
+        mms(w, [(T[bk][:, 0:w], T["SN" + x][0:n, :], T.E[0:n, 16 * lo:16 * hi], True, False)], ["SN" + x, "E"], bk)
+        st = min(CFG["tp"], hi - lo)
+        for a in range(lo, hi, st):
+            pick(16 * st, T.D[:, 16 * a:16 * (a + st)], T.TG[:, 0:2112].indirect(T["HU" + x][:, a:a + st]), TG + ["HU" + x],
+                 parts("D")[a // 16:(a + st) // 16], qs)
+        mms(w, [(T[bk][:, 0:w], T.IB[:], T.D[:, 16 * lo:16 * hi], False, True)], ["IB"] + parts("D")[lo // 16:hi // 16], bk)
+        op("s", lambda q: S.activation(T.R[:, 16 * lo:16 * hi], T[bk][:, 0:w], Act.Abs), w, [], ["R.%d" % (lo // 32)], [bk])
+
+    def cost(lo, hi, K):
+        R = ["R.%d" % c for c in range(lo // 32, (hi + 31) // 32)]
+        mms(16 * (hi - lo), [(T[K][lo:hi, m:264:33], T.R[:, 16 * lo + m:16 * hi:16], T.B1[:], True, True) for m in range(16)],
+            R + ["B1"], K)
+
+    def best_event(n, x):
+        na = n // 16
+        K, KS, EQ, HS, Z, OE = [nm + x for nm in ("PK", "KS", "EQ", "HS", "Z3", "OE")]
+        scan(264, T[KS][0:n, :], T.C1[0:n, :], T[K][0:n, 0:264], add, mn, ["C1"], [KS], [K])
+        tt(247, T[EQ][0:n, 0:247], T[K][0:n, 0:247], T[KS][0:n, 17:264], Op.is_equal, [KS], [EQ], [K])
+        tt(247, T[HS][0:n, 0:247], T.PH[0:n, 0:247], T[EQ][0:n, 0:247], mul, [EQ], [HS], ["PH"])
+        scan(256, T[Z][0:n, 0:256], T.C2[0:n, 0:256], T[HS][0:n, 0:256], mul, add, ["C2", HS], [Z])
+        items = []
+        for gg in range(8):
+            w = slice(112 - 16 * gg, 240 - 16 * gg)
+            items.append((T.PO[:, 0:na], T.LMP[0:n, w], T[Z][0:n, 33 * gg + 16:33 * gg + 16 + na], gg == 0, False))
+            items.append((T.PO[:, 0:na], T.LMN[0:n, w], T[Z][0:n, 33 * gg + 17:33 * gg + 17 + na], False, gg == 7))
+        mms(1024, items, ["LMP", "LMN", Z], "PO")
+        ts(1, T[OE][:, 0:na], T.PO[:, 0:na], 4096.0, 2048.0, mul, add, [], [OE], ["PO"])
+
+    PS = T.PM[:, 256:257]
+
+    def own_lookup(t):
+        learn = t < ST - 1
+        top, low, ends = T.MX[:, 15::16], T.MN[:, 15::16], parts("MX", 4) + parts("MN", 4)
+        hashes(128, top, low, ends, "")
+        if learn:
+            tt(256, T.SG[:, 0:128], top, low, sub, ends, ["SG"])
+        events_by_centre(128, "HI")
+        if t == 0:
+            mms(256, [(T.PK[:, 17:264:33], T.ONE[:, 0:128], T.TH8[:], True, True)], ["ONE", "TH8"], "PK")
+        for c, bk in enumerate(("PD0", "PD1", "PM", "PU")):
+            distances(128, 32 * c, 32 * c + 32, bk, "", CFG["tags"][c])
+            cost(32 * c, 32 * c + 32, "PK")
+        if t > 0:
+            ow, rb = "OW%d" % (t - 1), "RB%d" % (t - 1)
+            cp(48 * SC, T.EF[:, 0:2112].indirect(T[ow][:, 0:3]), T[rb][:], [ow, rb], EF)
+        best_event(128, "")
+        if learn:
+            ts(1, T.OF[:], T.PO[:, 0:8], -1.0 / 8192, None, Op.is_gt, None, [], ["OF"], ["PO"])
+        tt(128 * GA, T.VE[:], T.EF[:, 0:2112].indirect(T.OE[:]), T.BASE[:], add, EF + ["OE", "BASE"], ["VE"])
+        ts(128, T.OS[:], T.VE[:], 1.0 / 16, -15.0 / 32, mul, add, ["VE"], ["OS"])
+
+    def next_class():
+        ts(1, T.CC[:], T.KS[:, 16::33], MAGIC, MAGIC, add, sub, ["KS"], ["CC"])
+        op("v", lambda q: V.tensor_reduce(T.RC[:, 0:1], T.CC[:], AxisListType.X, add), 1, ["CC"], ["RC"])
+        mms(256, [(PS, T.ONE[:, 0:128], T.RC[:, 0:1], True, True)], ["ONE", "RC"], "PM")
+        ts(1, T.QI[:, 0:1], PS, 1.0 / 16, -15.0 / 32, mul, add, [], ["QI"], ["PM"])
+        ts(1, T.NC[:, 0:1], T.QI[:, 0:1], 16.0, PS, mul, sub, ["QI"], ["NC"], ["PM"])
+        ts(1, T.OC[:], T.I8S[:], T.NC[:, 0:1], 128.0, sub, mul, ["I8S", "NC"], ["OC"])
+        class_lists(128 * GA, T.NB[:, 0:2048].indirect(T.OC[:]), ["NB", "OC"])
+
+    def ask(t):
+        sc = "SC%d" % t
+        cp(128 * GA, T.FL[:], T.J[:, 0:8].indirect(T.OF[:]), ["J", "OF"], ["FL"])
+        scan(64, T.CN[:], T.RS[:, 0:128], T.FL[:], mul, add, ["RS", "FL"], ["CN"])
+        for a in range(3):
+            ts(64, T.LE[:, 128 * a:128 * a + 128], T.CN[:], T.I8[:, a:a + 1], None, Op.is_le, None, ["CN", "I8"], ["LE%d" % a])
+        scan(192, T.LS[:], T.RS[:], T.LE[:], mul, add, ["RS", "LE0", "LE1", "LE2"], ["LS"])
+        cp(1, T.L1[:, 0:3], T.LS[:, 127::128], ["LS"], ["L1"])
+        cp(48 * GA, T[sc][:], T.SG[:, 0:144].indirect(T.L1[:, 0:3]), ["SG", "SGb", "L1"], [sc])
+        send((rank + 1 + t) % N, "RQ%d" % t, sc, "rq%d" % t, "sq%d" % t)
+
+    def writers(t):
+        ts(48 * GA, T.HC[:], T.HI[:, 0:136].indirect(T.L1[:, 0:3]), -2048.0, 1.0 / 4096, add, mul, ["HI", "HIb", "L1"], ["HC"])
+        items = []
+        for a in range(3):
+            out = T.PM[:, 49 * a + 1:49 * a + 49]
+            items.append((out, T.P0[:], T.HC[:], True, False))
+            items.append((out, T.IB[:], T.MASK[:, 48 * a:48 * a + 48], False, True))
+        for b in range(16):
+            items.append((T.PM[:, 200:203], T.SEL[:, 15 - b:143 - b], T.HC[:, b:48:16], b == 0, b == 15))
+        mms(64 * 22, items, ["P0", "HC", "IB", "SEL", "MASK0", "MASK1", "MASK2"], "PM")
+        for a in range(3):
+            col = T.PM[:, 200 + a:201 + a]
+            ts(48, T.VAL[:, 49 * a + 1:49 * a + 49], T.PM[:, 49 * a + 1:49 * a + 49], col, col, Op.is_equal, add, [], ["VAL%d" % a], ["PM"])
+        scan(147, T.YS[:, 0:147], T.VAL[:, 0:147], T.CAP[:, 0:147], mx, mn,
+             ["VALz", "VAL0", "VAL1", "VAL2", "CAP0", "CAP1", "CAP2"], ["YS"])
+        ts(1, T["OW%d" % t][:, 0:3], T.YS[:, 48:147:49], 4096.0, 2048.0, mul, add, ["YS"], ["OW%d" % t])
+
+    def serve(t):
+        rq, an = "RQ%d" % t, "AN%d" % t
+        hashes(NQ, T[rq][:], None, [rq], "2")
+        events_by_centre(NQ, "HI2")
+        distances(NQ, 0, 32, "PD0", "2", CFG["far"][0])
+        distances(NQ, 32, 48, "PD1", "2", CFG["far"][1])
+        cost(0, NQ, "PK2")
+        best_event(NQ, "2")
+        ts(48 * GA, T.RI[:], T.EF[:, 0:2112].indirect(T.OE2[:, 0:3]), 16.0625, -15.0 / 32, mul, add, EF + ["OE2"], ["RI"])
+        ts(48, T[an][:], T.RI[:], 255, None, Op.bitwise_and, None, ["RI"], [an])
+        send((rank - 1 - t) % N, "RB%d" % t, an, "rb%d" % t, "sb%d" % t)
+
+    class_lists(128, T.NB0[:], ["NB0"])
+    for t in range(ST):
+        sites_in_class_order()
+        invert(t)
+        own_lookup(t)
+        gather("A2", "A", "OS")
+        if t == ST - 1:
+            k0 = 0
+            for k1 in CFG["out"]:
+                gather("X", "A2", "IV", k0, k1)
+                dma("y", T.y[:, 256 * k0:256 * k1], T.X[:, 256 * k0:256 * k1], 65536 * (k1 - k0), parts("X")[k0:k1], [])
+                k0 = k1
+            break
+        gather("X", "A2", "IV")
+        ask(t)
+        next_class()
+        writers(t)
+        serve(t)
+        cp(48 * SC, T.TG[:, 0:2112].indirect(T["OW%d" % t][:, 0:3]), T["SC%d" % t][:], ["OW%d" % t, "SC%d" % t], TG)
+
+    known = {q: {} for q in Q}
+    total = {}
+    wrote, readers, bank = {}, {}, {}
+    for t in range(ST - 1):
+        for name, src, rsem in (("RQ%d" % t, (rank - 1 - t) % N, "rq%d" % t), ("RB%d" % t, (rank + 1 + t) % N, "rb%d" % t)):
+            total[rsem] = len(topo.engines(T.cores[src], core))
+            wrote[name] = (rsem, total[rsem], {})
+
+    def need(q, events):
+        best = {}
+        for e in events:
+            if e[0] not in best or best[e[0]][1] < e[1]:
+                best[e[0]] = e
+        for key, val, snap in sorted(best.values(), key=lambda e: -len(e[2])):
+            if known[q].get(key, 0) < val:
+                Q[q].wait_ge(T.sem[key], val)
+                known[q][key] = val
+            for k2, v2 in snap.items():
+                if known[q].get(k2, 0) < v2:
+                    known[q][k2] = v2
+
+    ndma = 0
+    for k, q in schedule(ops):
+        o = ops[k]
+        ev = [wrote[r] for r in o["R"] + o["W"] if r in wrote]
+        for w in o["W"]:
+            ev.extend(readers.get(w, []))
+        for b in o["P"]:
+            ev.extend(e for q2, e in bank.get(b, {}).items() if q2 != q)
+        need(q, ev)
+        if o["kind"] == "c":
+            key = "c" + q
+            for ins in o["fn"](q):
+                ins.then_inc(T.sem[key], 1)
+                total[key] = total.get(key, 0) + 1
+        elif o["kind"] == "d":
+            key = "d%d" % ndma
+            ndma += 1
+            o["fn"](q).then_inc(T.sem[key], 16)
+            total[key] = 16
+        else:
+            o["fn"](q)
+            key = o["sem"][0]
+            total[key] = o["sem"][1]
+        e = (key, total[key], dict(known[q]))
+        for r in o["R"]:
+            readers.setdefault(r, []).append(e)
+        for w in o["W"]:
+            wrote[w] = e
+            readers[w] = []
+        for b in o["P"]:
+            bank.setdefault(b, {})[q] = e
+    need("y", [(key, val, {}) for key, val in sorted(total.items())])

@@ -1,46 +1,50 @@
 from concourse.mybir import AluOpType, AxisListType, ActivationFunctionType
 
 F, B, I, U, H = "float32", "bfloat16", "int32", "uint16", "float16"
+SG_W = 26
+KW = 8 * SG_W
 SCRATCH = {}
-for _n in ("X", "A", "A2", "MX", "MN", "E", "D", "R"):
+for _n in ("X", "A", "A2", "MX", "MN", "D", "R"):
     SCRATCH[_n] = ("sbuf", [128, 2048], B)
 for _n, _w, _d in (
-        ("SG", 144, B), ("SN", 128, B), ("IB", 128, B), ("IBN", 128, B),
+        ("SG", 144, B), ("SN", 128, B), ("IB", 128, B), ("IBN", 128, B), ("E", 512, B),
         ("TG", 2112, B), ("EF", 2112, B), ("NB", 2048, I), ("NB0", 128, I), ("IO", 2048, F), ("W32", 2048, F),
-        ("IVF", 128, F), ("IV", 128, U), ("NBU", 128, U), ("PHI", 128, I), ("PHA", 128, I), ("PHU", 128, U),
-        ("WW", 8, B), ("TH", 8, I), ("PI", 8, I), ("CI", 8, I), ("CF", 16, F), ("JG", 128, F),
-        ("J", 240, F), ("LMP", 240, H), ("LMN", 240, H),
-        ("RST", 512, B), ("BIG", 512, B), ("W1", 128, B), ("W2", 128, B), ("W1N", 128, B), ("W2N", 128, B), ("B1", 8, B),
-        ("TH8", 8, F), ("ONE", 264, F), ("ONB", 264, B), ("SPR", 264, B), ("C1", 264, F), ("C2", 264, F),
-        ("KS", 264, F), ("EQ", 264, F), ("HS", 264, F), ("Z3", 264, H), ("KS2", 264, F), ("EQ2", 264, F), ("HS2", 264, F), ("Z32", 264, H),
+        ("IVF", 128, F), ("IV", 128, U), ("PHI", 256, I), ("PHA", 256, I), ("L0", 128, U), ("L1S", 128, U), ("L2", 256, U),
+        ("WW", 8, B), ("TH", 8, I), ("PI", 8, I), ("CI", 8, B), ("CF", 16, F), ("JE", 512, B),
+        ("J", 240, B), ("LM", 456, H), ("LMN", 456, H), ("ZO", 512, B), ("CA", 128, B), ("CM", 128, B),
+        ("RST", 512, B), ("BIG", 512, B), ("W", 256, B), ("WN", 256, B), ("B1", 8, B),
+        ("TH8", 8, F), ("ONE", 128, F), ("KC", KW, B), ("C1", KW, B),
+        ("KS", KW, F), ("NE", KW, B), ("Z", KW, H), ("KS2", KW, F), ("NE2", KW, B), ("Z2", KW, H),
         ("BASE", 128, F), ("I8", 8, F), ("I8S", 8, F), ("RS", 384, B), ("P0", 128, B), ("SEL", 144, B),
-        ("MASK", 144, B), ("CAP", 152, F), ("VAL", 152, F), ("YS", 152, F),
-        ("UI", 256, I), ("UA", 256, I), ("U1", 128, F), ("PP", 128, I), ("HI", 136, I), ("HU", 128, U), ("HF", 128, H),
-        ("HI2", 48, I), ("UI2", 96, I), ("UA2", 96, I), ("U12", 48, F), ("PP2", 48, I), ("HU2", 48, U), ("SN2", 128, B),
+        ("L16", 128, B), ("MK", 144, B), ("CAP", 152, F), ("VAL", 152, F), ("YS", 152, F),
+        ("UQ", 256, F), ("UR", 256, F), ("PP", 128, I), ("HI", 136, I), ("HU", 128, U), ("HF", 128, H),
+        ("UQ2", 96, F), ("UR2", 96, F), ("PP2", 48, I), ("HI2", 48, I), ("HU2", 48, U), ("HF2", 48, H), ("SN2", 128, B),
         ("OE", 8, U), ("OF", 8, U), ("VE", 128, F), ("OS", 128, U), ("OE2", 8, U),
         ("CC", 8, F), ("RC", 8, F), ("QI", 8, I), ("NC", 8, F), ("OC", 8, U),
         ("FL", 128, B), ("CN", 128, B), ("LE", 384, B), ("LS", 384, B), ("L1", 8, U), ("HC", 48, H),
         ("OW0", 8, U), ("OW1", 8, U), ("SC0", 48, B), ("SC1", 48, B), ("RQ0", 48, B), ("RQ1", 48, B),
         ("RI", 48, I), ("AN0", 48, I), ("AN1", 48, I), ("RB0", 48, I), ("RB1", 48, I)):
     SCRATCH[_n] = ("sbuf", [128, _w], _d)
-for _n in ("PU", "PK", "PK2", "PH", "PO", "PM", "PD0", "PD1"):
+for _n in ("PK", "PK2", "PA", "PB", "PD0", "PD1", "PD2", "PD3"):
     SCRATCH[_n] = ("psum", [128, 512], F)
 
 SEMAPHORES = ["cg", "cv", "cs", "ct", "rq0", "rq1", "rb0", "rb1", "sq0", "sq1", "sb0", "sb1"] + ["d%d" % _i for _i in range(24)]
 
 ST, NQ = 3, 48
-MAGIC = 12582912.0
-CFG = {"cyc": 1.04e-3, "fix": 0.06, "wake": 0.3, "gather": 1.7, "scatter": 3.8, "pe": 0.52e-3, "dma": 2.0, "bw": 250e3,
-       "remote": 4, "first": 3, "table": 1.3, "inv": "vs", "seed": 70299, "noise": 0.2, "piece": 2, "out": [2, 4, 6, 8],
-       "spare": 0.4, "rounds": 8, "tp": 16, "tags": ["s", "v", "vs", "v"], "far": ["vs", "vs"],
-       "tweaks": [(0, 0.3), (35, -3), (36, -3), (37, -3), (38, -3), (49, -1), (86, -3), (87, -3), (88, -3), (89, -3), (139, 3),
-                  (175, -3), (176, -3), (177, -3), (178, -3), (307, 3), (308, 2), (309, -1), (310, -1), (311, -1), (373, -3),
-                  (374, -3), (375, -3), (376, -3), (391, -1), (392, -1)],
-       "force": {81: "s", 356: "v", 102: "s"}}
+ROUND = 1.5 * 2.0 ** 34
+HUGE = 2.0 ** 20
+MODELS = (
+    {"f": 1.08, "ga": 1.56, "sc": 3.6, "fix": 0.03, "wake": 0.1, "dma": 1.0, "bw": 350e3, "rem": 1.6, "first": 1.5},
+    {"f": 1.0, "ga": 1.4, "sc": 2.8, "fix": 0.05, "wake": 0.2, "dma": 1.5, "bw": 300e3, "rem": 2.5, "first": 2.5},
+    {"f": 1.4, "ga": 1.9, "sc": 5.0, "fix": 0.03, "wake": 0.1, "dma": 1.0, "bw": 350e3, "rem": 2.0, "first": 2.0},
+)
+CFG = {"piece": 2, "inv": 1, "tp": 16, "out": [4, 6, 8], "seed": 1, "tries": 150000, "tight": 0.1, "heat": 0.6}
+CYC, PECYC = 0.83e-3, 0.417e-3
+MEMO = {}
 
 
 def schedule(ops):
-    n, wake = len(ops), CFG["wake"]
+    n = len(ops)
     pred = [set() for _ in ops]
     wrote, readers, bank = {}, {}, {}
     for k, o in enumerate(ops):
@@ -61,64 +65,160 @@ def schedule(ops):
             wrote[w] = k
             readers[w] = []
         pred[k].discard(k)
+    pred = [sorted(p) for p in pred]
     succ = [[] for _ in ops]
     for k in range(n):
         for p in pred[k]:
             succ[p].append(k)
 
-    def gap(p, y):
-        return ops[p]["late"] + (0.0 if ops[p]["qs"] == ops[y]["qs"] == "t" else wake)
+    def times(m):
+        busy, late, sends = [], [], 0
+        for o in ops:
+            fix, plain, ga, sc = o["cost"]
+            if o["kind"] == "c":
+                busy.append(m["f"] * (fix + CYC * (plain + ga * m["ga"] + sc * m["sc"])) + (m["fix"] if plain and not fix else 0.0))
+                late.append(0.0)
+            elif o["kind"] == "d":
+                busy.append(0.06)
+                late.append(m["dma"] + plain / m["bw"])
+            else:
+                busy.append(0.5)
+                late.append(m["rem"] + (0.0 if sends else m["first"]))
+                sends += 1
+        lag = [[late[p] + (0.0 if ops[p]["qs"] == ops[k]["qs"] == "t" else m["wake"]) for p in pred[k]] for k in range(n)]
+        return busy, late, lag
 
-    def sweep(prio, back, force=None):
-        before, behind = (succ, pred) if back else (pred, succ)
-        left = [len(b) for b in before]
-        ready = [k for k in range(n) if not left[k]]
+    costs = [times(m) for m in MODELS]
+
+    QI = {q: i for i, q in enumerate("gvsty")}
+    rows = [[(p, costs[0][2][k][j], costs[1][2][k][j], costs[2][2][k][j]) for j, p in enumerate(pred[k])] for k in range(n)]
+    dur = [(costs[0][0][k], costs[1][0][k], costs[2][0][k]) for k in range(n)]
+    tail = [k for k in range(n) if not succ[k]]
+    moved = [[ops[k]["cost"][1] / m["bw"] for m in MODELS] if ops[k]["kind"] == "d" else None for k in range(n)]
+    wa, wb, wc = [1.0 / m["f"] for m in MODELS]
+
+    def worth(order, where):
+        fa, fb, fc = [0.0] * 5, [0.0] * 5, [0.0] * 5
+        da, db, dc = [0.0] * n, [0.0] * n, [0.0] * n
+        lane = [0.0] * 3
+        for k in order:
+            q = where[k]
+            a, b, c = fa[q], fb[q], fc[q]
+            for p, la, lb, lc in rows[k]:
+                la += da[p]
+                if la > a:
+                    a = la
+                lb += db[p]
+                if lb > b:
+                    b = lb
+                lc += dc[p]
+                if lc > c:
+                    c = lc
+            u = dur[k]
+            fa[q] = da[k] = a + u[0]
+            fb[q] = db[k] = b + u[1]
+            fc[q] = dc[k] = c + u[2]
+            if moved[k]:
+                for i, (s, d) in enumerate(((a, da), (b, db), (c, dc))):
+                    lane[i] = max(lane[i], s + MODELS[i]["dma"]) + moved[k][i]
+                    d[k] = max(d[k], lane[i] - costs[i][1][k])
+        end = sum(w * max(d[k] + c[1][k] for k in tail) for w, d, c in ((wa, da, costs[0]), (wb, db, costs[1]), (wc, dc, costs[2])))
+        return end + CFG["tight"] * (sum(da) + sum(db)) / n
+
+    def sweep(prio, bias):
+        busy, late, lag = costs[0]
+        left = [len(b) for b in pred]
+        ready = [(prio[k], k) for k in range(n) if not left[k]]
         taken = {q: [] for q in "gvsty"}
         start, where = [0.0] * n, [""] * n
         while ready:
-            k = min(ready, key=lambda j: (prio[j], j))
-            ready.remove(k)
-            can = ops[k]["late"] if back else 0.0
-            for p in before[k]:
-                can = max(can, start[p] + ops[p]["busy"] + (gap(k, p) if back else gap(p, k)))
+            e = min(ready)
+            ready.remove(e)
+            k = e[1]
+            can, b = 0.0, busy[k]
+            for p, g_ in zip(pred[k], lag[k]):
+                if start[p] + busy[p] + g_ > can:
+                    can = start[p] + busy[p] + g_
             best = None
-            for q in (force or {}).get(k, ops[k]["qs"]):
-                s, at = can, 0
-                for a, b in taken[q]:
-                    if s + ops[k]["busy"] <= a + 1e-9:
-                        break
-                    s = max(s, b)
+            for q in ops[k]["qs"]:
+                t, s = taken[q], can
+                at = len(t)
+                while at and t[at - 1][1] > can:
+                    at -= 1
+                while at < len(t) and s + b > t[at][0] + 1e-9:
+                    s = max(s, t[at][1])
                     at += 1
-                s_cmp = s + (CFG["spare"] if q == "v" else 0.0)
+                s_cmp = s + (bias[k] if q == "v" else 0.0)
                 if best is None or s_cmp < best[0]:
                     best = (s_cmp, s, q, at)
             _, s, q, at = best
-            taken[q].insert(at, (s, s + ops[k]["busy"]))
+            taken[q].insert(at, (s, s + b))
             start[k], where[k] = s, q
-            for y in behind[k]:
+            for y in succ[k]:
                 left[y] -= 1
                 if not left[y]:
-                    ready.append(y)
-        end = max(start[k] + ops[k]["busy"] + (0.0 if back else ops[k]["late"]) for k in range(n))
-        return start, where, end
+                    ready.append((prio[y], y))
+        order = [(k, where[k]) for k in sorted(range(n), key=lambda j: (start[j], j))]
+        return order, start
 
-    x = 12345 + 977 * CFG["seed"]
+    x = [12345 + 977 * CFG["seed"]]
+
+    def rnd():
+        x[0] = (x[0] * 1103515245 + 12345) % 2147483648
+        return x[0] / 2147483648
+
+    busy, late, lag = costs[0]
     prio = [0.0] * n
     for k in reversed(range(n)):
-        x = (x * 1103515245 + 12345) % 2147483648
-        prio[k] = min([prio[y] - gap(k, y) for y in succ[k]] + [-ops[k]["late"]]) - ops[k]["busy"] - CFG["noise"] * x / 2147483648
-    best = None
-    for _ in range(CFG["rounds"]):
-        start, where, end = sweep(prio, False)
-        if best is None or end < best[2]:
-            best = (start, where, end)
-        late, _w, _e = sweep([-(start[k] + ops[k]["busy"]) for k in range(n)], True)
-        prio = [-(late[k] + ops[k]["busy"]) for k in range(n)]
-    prio = list(best[0])
-    for k, d in CFG["tweaks"]:
-        prio[k] += d
-    start, where, end = sweep(prio, False, CFG["force"])
-    return [(k, where[k]) for k in sorted(range(n), key=lambda j: (start[j], j))]
+        prio[k] = min([prio[k], -late[k]]) - busy[k]
+        for p, g_ in zip(pred[k], lag[k]):
+            prio[p] = min(prio[p], prio[k] - g_)
+    first, start = sweep(prio, [0.3] * n)
+    order, where = [k for k, q in first], [0] * n
+    for k, q in first:
+        where[k] = QI[q]
+    now = worth(order, where)
+    best = (now, order, where)
+    either = [k for k in range(n) if len(ops[k]["qs"]) > 1]
+    tries = CFG["tries"]
+    for it in range(tries):
+        o2, w2 = order, where
+        z = rnd()
+        if z < 0.2:
+            k = either[int(rnd() * len(either))]
+            w2 = list(where)
+            other = [QI[q] for q in ops[k]["qs"] if QI[q] != where[k]]
+            w2[k] = other[int(rnd() * len(other))]
+            i = order.index(k)
+        else:
+            i = int(rnd() * n)
+            k = order[i]
+        if z > 0.1:
+            hops, step = 1 + int(5 * rnd() * rnd()), (-1 if rnd() < 0.5 else 1)
+            j = i
+            while hops and 0 <= j + step < n:
+                j += step
+                hops -= w2[order[j]] == w2[k]
+            links = pred if step < 0 else succ
+            span = order[j:i + 1][::-1] if step < 0 else order[i:j + 1]
+            tied, go, stay = set(links[k]), [k], []
+            for y in span[1:]:
+                if y in tied:
+                    go.append(y)
+                    tied.update(links[y])
+                else:
+                    stay.append(y)
+            if step < 0:
+                o2 = order[:j] + go[::-1] + stay[::-1] + order[i + 1:]
+            else:
+                o2 = order[:i] + stay + go + order[j + 1:]
+        w = worth(o2, w2)
+        if w <= now + CFG["heat"] * (1.0 - it / tries) * rnd() ** 3:
+            now, order, where = w, o2, w2
+            if w < best[0]:
+                best = (w, o2, w2)
+    MEMO["worth"] = best[0]
+    return [(k, "gvsty"[best[2][k]]) for k in best[1]]
 
 
 def rank_program(g, core, T, topo):
@@ -132,29 +232,27 @@ def rank_program(g, core, T, topo):
     V, S, PE = g.vector, g.scalar, g.tensor
     ops = []
 
-    def record(kind, qs, fn, R, W, P, busy, late=0.0, after=(), marks=(), sem=None):
-        ops.append(dict(kind=kind, qs=qs, fn=fn, R=list(R), W=list(W), P=list(P), busy=busy, late=late, after=list(after),
+    def record(kind, qs, fn, R, W, P, cost, after=(), marks=(), sem=None):
+        ops.append(dict(kind=kind, qs=qs, fn=fn, R=list(R), W=list(W), P=list(P), cost=cost, after=list(after),
                         marks=list(marks), sem=sem))
 
-    def cyc(n):
-        return max(n, 64) * CFG["cyc"] + CFG["fix"]
+    def cost_of(n):
+        if isinstance(n, tuple):
+            return (0.058 + (n[2] if len(n) > 2 else 0.0), 0, n[1] if n[0] == "g" else 0, n[1] if n[0] == "s" else 0)
+        return (0.0, max(n, 64), 0, 0)
 
-    def op(qs, fn, n, R, W, P=(), table=False):
+    def op(qs, fn, n, R, W, P=()):
         after = ["sent." + r for r in R if r[:2] in ("RQ", "RB")]
-        record("c", qs, lambda q: [fn(q)], R, W, P, cyc(n) + (CFG["table"] if table else 0.0), after=after)
+        record("c", qs, lambda q: [fn(q)], R, W, P, cost_of(n), after=after)
 
-    def dma(q, out, in_, nbytes, R, W, more=0.0):
-        record("d", q, lambda q: Q[q].dma_start(out, in_), R, W, (), 0.1, CFG["dma"] + nbytes / CFG["bw"] + more)
-
-    sent = [0]
+    def dma(q, out, in_, nbytes, R, W):
+        record("d", q, lambda q: Q[q].dma_start(out, in_), R, W, (), (0, nbytes, 0, 0))
 
     def send(dst_rank, name, src, rsem, lsem):
         dst = T.cores[dst_rank]
         rid, pid, _ = topo.addr(dst)
         record("r", "g", lambda q: g.remote_dma(T[name][:], T[src][:], T.sem[rsem], T.sem[lsem], pid, rid, topo.mask(core, dst)),
-               [src], [], (), 0.5, CFG["remote"] + (0.0 if sent[0] else CFG["first"]), marks=["sent." + name],
-               sem=(lsem, len(topo.engines(core, dst))))
-        sent[0] = 1
+               [src], [], (), (0, 0, 0, 0), marks=["sent." + name], sem=(lsem, len(topo.engines(core, dst))))
 
     def ts(n, out, in0, s1, s2, o0, o1, R, W, P=()):
         if o1 is None:
@@ -176,10 +274,10 @@ def rank_program(g, core, T, topo):
 
     def mms(n, items, R, bk):
         after = ["sent." + r for r in R if r[:2] == "RQ"]
-        record("c", "t", lambda q: [PE.matmul(*it) for it in items], R, [], [bk], n * CFG["pe"], after=after)
+        record("c", "t", lambda q: [PE.matmul(*it) for it in items], R, [], [bk], (n * PECYC, 0, 0, 0), after=after)
 
     def gp(fn, n, R, W):
-        record("c", "g", lambda q: [fn()], R, W, (), 0.17 + 2 * n * CFG["cyc"])
+        record("c", "g", lambda q: [fn()], R, W, (), (0.15, 2 * n, 0, 0))
 
     def iota(n, out, pat, base, cm, W, flt=True):
         if flt:
@@ -190,19 +288,14 @@ def rank_program(g, core, T, topo):
     def asel(n, out, in_, pat, cmp, base, cm, R, W, other=0.0):
         gp(lambda: g.affine_select(out, in_, pat, cmp, other, base, cm), n, R, W)
 
-    def gfill(out, n, c, W):
-        asel(n, out, T.ONE[:, 0:n], [[0, n]], Op.is_equal, 1, 0, ["ONE"], W, c)
-
     def parts(name, n=8):
         return ["%s.%d" % (name, k) for k in range(n)]
-
-    GA, SC = CFG["gather"], CFG["scatter"]
 
     def copy(q, out, in_):
         return V.tensor_copy(out, in_) if q == "v" else S.activation(out, in_, Act.Copy)
 
     def pick(n, out, win, R, W, qs="vs"):
-        op(qs, lambda q: copy(q, out, win), n * GA, R, W)
+        op(qs, lambda q: copy(q, out, win), ("g", n), R, W)
 
     def gather(dst, src, off, k0=0, k1=8):
         w = CFG["piece"]
@@ -210,107 +303,94 @@ def rank_program(g, core, T, topo):
             pick(256 * w, T[dst][:, 256 * k:256 * (k + w)], T[src][:, 0:2048].indirect(T[off][:, 16 * k:16 * (k + w)]),
                  parts(src) + [off], parts(dst)[k:k + w])
 
-    cR, cG, cM, cT, cW1, cW2, cN1, cN2 = [T.CF[:, k:k + 1] for k in range(8)]
-    cL = T.CF[:, 12:13]
+    cR, cG, c32, cP = [T.CI[:, k:k + 1] for k in range(4)]
+    cT, cK = T.CF[:, 0:1], T.CF[:, 1:2]
+    ones, zeros = T.ZO[:, 0:256], T.ZO[:, 256:512]
+    JG = T.JE[:, 0:128]
+    LMP, SPR = T.LM[:, 0:240], T.LM[:, 240:240 + KW]
 
     c0 = rank % 16
     dma("s", T.NB0[:], T.nb[:, 128 * c0:128 * c0 + 128], 65536, [], ["NB0"])
     dma("y", T.X[:], T.x[:], 524288, [], parts("X"))
-    dma("s", T.WW[:, 0:2], T.w[:], 0, [], ["WW"])
-    dma("y", T.TG[:, 0:2048], T.tag[:], 524288, ["X.0"], ["TGa"])
-    dma("y", T.TH[:, 0:1], T.th[:], 0, ["X.0"], ["TH"])
-    dma("y", T.EF[:, 0:2048], T.ef[:], 524288, ["X.0"], ["EFa"], 2.0)
-    dma("y", T.NB[:], T.nb[:], 1048576, ["TGa"], ["NB"])
-    TG, EF = ["TGa", "TGb"], ["EFa", "EFb"]
+    dma("y", T.WW[:, 0:2], T.w[:], 8192, [], ["WW"])
+    dma("y", T.TG[:, 0:2048], T.tag[:], 524288, ["X.0"], ["TG"])
+    dma("y", T.TH[:, 0:1], T.th[:], 8192, ["X.0"], ["TH"])
+    dma("y", T.EF[:, 0:2048], T.ef[:], 524288, ["TG"], ["EFa"])
+    dma("y", T.NB[:], T.nb[:], 1048576, ["EFa"], ["NB"])
+    EF = ["EFa", "EFb"]
 
-    fill(1024, T.E[:], 1.0, ["E"])
-    fill(132, T.ONB[:], 1.0, ["ONB"])
-    iota(1, T.PI[:, 0:1], [[0, 1]], 0, 1, ["PI"], False)
-    iota(128, T.JG[:], [[1, 8], [0, 16]], 0, 0, ["JG"])
-    iota(512, T.IO[:, 0:512], [[1, 512]], 64, 0, ["IO.0"])
-    asel(128, T.IB[:], T.ONB[:, 0:128], [[-1, 128]], Op.is_equal, 0, 1, ["ONB"], ["IB"])
-    asel(2048, T.E[:], T.E[:], [[-1, 128], [0, 16]], Op.is_equal, 0, 1, ["E"], ["E"])
-    iota(264, T.ONE[:], [[0, 264]], 1, 0, ["ONE"])
-    asel(264, T.SPR[:], T.ONB[:], [[-16, 8], [-1, 33]], Op.is_equal, 0, 1, ["ONB"], ["SPR"])
-    asel(264, T.SPR[:], T.SPR[:], [[0, 8], [-1, 33]], Op.is_ge, 15, 0, ["SPR"], ["SPR"])
-    gfill(T.C1[:], 264, -1.0 / 16, ["C1"])
-    gfill(T.C1[:, 0::33], 8, 1.0e6, ["C1"])
-    gfill(T.C1[:, 16::33], 8, 15.0 / 32, ["C1"])
-    gfill(T.C1[:, 17::33], 8, 15.0 / 32, ["C1"])
-    asel(264, T.C2[:], T.ONE[:], [[0, 8], [-16, 33]], Op.is_ge, 256, 1, ["ONE"], ["C2"])
-    iota(8, T.C2[:, 0::33], [[0, 8]], 0, 0, ["C2"])
-    iota(24, T.HS[:, 240:264], [[0, 24]], 0, 0, ["HS"])
-    iota(24, T.HS2[:, 240:264], [[0, 24]], 0, 0, ["HS2"])
+    fill(128, ones, 1.0, ["ones"])
+    fill(128, zeros, 0.0, ["zeros"])
+    iota(1, T.PI[:, 3:4], [[0, 1]], 0, 1, ["PI3"], False)
+    iota(256, T.IO[:, 0:256], [[1, 256]], 64, 0, ["IO.0"])
+    op("s", lambda q: S.activation(T.IO[:, 256:512], T.IO[:, 0:256], Act.Silu, 256.0), 256 + 1500, ["IO.0"], ["IO.1", "table"])
+    for c in range(1, 4):
+        iota(512, T.IO[:, 512 * c:512 * c + 512], [[1, 512]], 64 + 512 * c, 0, parts("IO")[2 * c:2 * c + 2])
+    iota(128, JG, [[1, 8], [0, 16]], 0, 0, ["JG"])
+    iota(384, T.JE[:, 128:512], [[1, 24], [0, 16]], 8, 0, ["JE"])
+    asel(128, T.IB[:], T.ZO[:, 256:384], [[-1, 128]], Op.not_equal, 0, 1, ["zeros"], ["IB"], 1.0)
+    asel(128, T.IBN[:], T.ZO[:, 256:384], [[-1, 128]], Op.not_equal, 0, 1, ["zeros"], ["IBN"], -1.0)
+    iota(128, T.CA[0:2, :], [[0, 128]], -1024, 0, ["CA"])
+    asel(128, T.CA[0:2, :], T.CA[0:2, :], [[0, 128]], Op.is_equal, 0, 1, ["CA"], ["CA"], 0.5)
+    iota(128, T.CM[0:1, :], [[0, 8], [64, 16]], 32, 0, ["CM"])
     iota(240, T.J[:], [[1, 240]], 0, 0, ["J"])
+    asel(KW, T.KC[:], T.ZO[:, 0:KW], [[0, 8], [16, SG_W]], Op.is_ge, -273, -1, ["ones"], ["KC"], -HUGE)
+    asel(KW, T.C1[:], T.ZO[:, 256:256 + KW], [[0, 8], [1, SG_W]], Op.not_equal, 0, 0, ["zeros"], ["C1"], HUGE)
     iota(128, T.BASE[:], [[256, 128]], 0, 0, ["BASE"])
+    iota(128, T.ONE[:], [[0, 128]], 1, 0, ["ONE"])
     iota(384, T.RS[:], [[0, 384]], 1, 0, ["RS"])
     iota(3, T.RS[:, 0::128], [[0, 3]], 0, 0, ["RS"])
     iota(16, T.SG[:, 128:144], [[0, 16]], 0, 0, ["SGb"])
     iota(8, T.HI[:, 128:136], [[0, 8]], 6144, 0, ["HIb"], False)
-    asel(128, T.P0[:], T.ONB[:, 0:128], [[-16, 8], [0, 16]], Op.is_equal, 0, 1, ["ONB"], ["P0"])
+    asel(128, T.P0[:], T.ZO[:, 0:128], [[-16, 8], [0, 16]], Op.is_equal, 0, 1, ["ones"], ["P0"])
     iota(144, T.SEL[:], [[0, 144]], 0, 0, ["SEL"])
-    asel(8, T.SEL[:, 15:143:16], T.ONB[:, 0:8], [[-16, 8]], Op.is_equal, 0, 1, ["ONB"], ["SEL"])
+    asel(8, T.SEL[:, 15:143:16], T.ZO[:, 0:8], [[-16, 8]], Op.is_equal, 0, 1, ["ones"], ["SEL"])
+    asel(128, T.L16[0:16, :], T.ZO[0:16, 0:128], [[0, 8], [-1, 16]], Op.is_equal, 0, 1, ["ones"], ["L16"])
+    asel(144, T.MK[0:16, :], T.ZO[0:16, 0:144], [[-16, 3], [1, 48]], Op.is_ge, 0, -1, ["ones"], ["MK"])
     iota(3, T.VAL[:, 0:147:49], [[0, 3]], 0, 0, ["VALz"])
-
-    def positions(c):
-        op("s", lambda q: S.activation(T.IO[:, 512 * c:512 * c + 512], T.IO[:, 0:512], Act.Identity, 512.0 * c), 512,
-           ["IO.0"], ["IO.%d" % c])
-    for c in range(1, 4):
-        positions(c)
+    iota(147, T.CAP[:, 0:147], [[0, 147]], 4, 0, ["CAP"])
+    iota(3, T.CAP[:, 0:147:49], [[0, 3]], -1, 0, ["CAP"])
 
     fill(256, T.RST[:], 1.0, ["RST"])
     fill(256, T.BIG[:], 0.0, ["BIG"])
-    ts(1, T.CI[:, 0:1], T.PI[:, 0:1], 15, None, Op.bitwise_and, None, ["PI"], ["CI0"])
-    ts(1, T.CI[:, 1:2], T.PI[:, 0:1], 4, None, Op.arith_shift_right, None, ["PI"], ["CI1"])
     fill(1, T.RST[:, 0::16], 0.0, ["RST"])
     fill(1, T.BIG[:, 0::16], 256.0, ["BIG"])
-    cp(1, T.CF[:, 0:2], T.CI[:, 0:2], ["CI0", "CI1"], ["cR"])
-    fill(1, T.TG[:, 2048:2112], 0.0, ["TGb"])
-    fill(1, T.EF[:, 2048:2112], 0.0, ["EFb"])
-    ts(1, cM, cR, 64.0, 32.0, mul, add, ["cR"], ["cM"])
-    ts(1, T.B1[:], T.JG[:, 0::16], cG, None, Op.is_equal, None, ["JG", "cR"], ["B1"])
-    cp(1, T.CF[:, 4:6], T.WW[:, 0:2], ["WW"], ["cW"])
-    ts(1, T.CF[:, 6:8], T.WW[:, 0:2], -1.0, None, mul, None, ["WW"], ["cN"])
-    for nm, col in (("W1", cW1), ("W2", cW2), ("W1N", cN1), ("W2N", cN2)):
-        ts(128, T[nm][:], T.JG[:], cG, col, Op.is_equal, mul, ["JG", "cR", "cW", "cN"], [nm])
-    ts(1, T.IBN[:], T.IB[:], -1.0, None, mul, None, ["IB"], ["IBN"])
-    fill(264, T.PK[:, 0:264], 1.0e6, [], ["PK"])
-    fill(264, T.PK2[:, 0:264], 1.0e6, [], ["PK2"])
-    ts(1, cT, T.TH[:, 0:1], 31.0 / 32, 1.0 / 16, add, mul, ["TH"], ["cT"])
-    ts(1, cL, cR, 112.0, None, add, None, ["cR"], ["cL"])
-    ts(1, T.TH8[:], T.JG[:, 0::16], cG, cT, Op.is_equal, mul, ["JG", "cR", "cT"], ["TH8"])
-    ts(240, T.LMP[:], T.J[:], cL, None, Op.is_equal, None, ["J", "cL"], ["LMP"])
-    ts(120, T.LMN[:], T.LMP[:], -1.0, None, mul, None, ["LMP"], ["LMN"])
+    ts(1, T.PI[:, 0:1], T.PI[:, 3:4], 15, None, Op.bitwise_and, None, ["PI3"], ["PI0"])
+    ts(1, T.PI[:, 1:2], T.PI[:, 3:4], 4, None, Op.arith_shift_right, None, ["PI3"], ["PI1"])
+    ts(1, T.PI[:, 2:3], T.PI[:, 3:4], 31, None, Op.bitwise_and, None, ["PI3"], ["PI2"])
+    cp(1, T.CI[:, 0:4], T.PI[:, 0:4], ["PI0", "PI1", "PI2", "PI3"], ["cR"])
+    for k in range(2):
+        ts(64, T.W[:, 128 * k:128 * k + 128], JG, cG, T.WW[:, k:k + 1], Op.is_equal, mul, ["JG", "cR", "WW"], ["W%d" % k])
+    ts(128, T.WN[:], T.W[:], -1.0, None, mul, None, ["W0", "W1"], ["WN"])
+    ts(1, T.B1[:], T.JE[:, 0:128:16], cG, None, Op.is_equal, None, ["JG", "cR"], ["B1"])
+    ts(256, T.E[:], T.JE[:], c32, None, Op.is_equal, None, ["JG", "JE", "cR"], ["E"])
+    ts(1, cT, T.TH[:, 0:1], 0.5, 1.0 / 16, add, mul, ["TH"], ["cT"])
+    ts(1, T.TH8[:], T.B1[:], cT, None, mul, None, ["B1", "cT"], ["TH8"])
+    ts(1, cK, cG, 10.0, cP, mul, add, ["cR"], ["cK"])
+    ts(120, LMP, T.J[:], cR, 112.0, sub, Op.is_equal, ["J", "cR"], ["LMP"])
+    ts(108, T.LM[:, 240:456], T.J[:, 0:216], cK, 1.0, sub, Op.is_equal, ["J", "cK"], ["SPR"])
+    ts(228, T.LMN[:], T.LM[:], -1.0, None, mul, None, ["LMP", "SPR"], ["LMN"])
     ts(1, T.EF[:, 2048:2049], cR, 17.0, None, mul, None, ["cR"], ["EFb"])
-    ts(1, T.I8[:], T.JG[:, 0::16], 16.0, cR, mul, add, ["JG", "cR"], ["I8"])
-    for a in range(3):
-        ts(1, T.MASK[:, 48 * a:48 * a + 48], T.J[:, 0:48], T.I8[:, a:a + 1], 2.0, Op.is_ge, mul, ["J", "I8"], ["MASK%d" % a])
+    ts(1, T.I8[:], T.JE[:, 0:128:16], 16.0, cR, mul, add, ["JG", "cR"], ["I8"])
     ts(1, T.I8S[:], T.I8[:], 1.0 / 128, None, mul, None, ["I8"], ["I8S"])
-    ts(1, T.CF[:, 8:11], T.I8[:, 0:3], 16.0, 1.0 / 4096, add, mul, ["I8"], ["cC"])
-    for a in range(3):
-        ts(1, T.CAP[:, 49 * a:49 * a + 49], T.J[:, 0:49], 0.0, T.CF[:, 8 + a:9 + a], mul, add, ["J", "cC"], ["CAP%d" % a])
-    fill(1, T.CAP[:, 0:147:49], -1.0, ["CAP0", "CAP1", "CAP2"])
+    ts(1, T.CAP[:, 48:147:49], T.I8[:, 0:3], 16.0, 1.0 / 4096, add, mul, ["I8"], ["CAP"])
+    for K in ("PK", "PK2"):
+        mms(KW, [(T[K][:, 0:KW], T.IBN[:], T.KC[:], True, True)], ["IBN", "KC"], K)
+    mms(256, [(T.PK[:, 17:KW:SG_W], T.ONE[:], T.TH8[:], True, True)], ["ONE", "TH8"], "PK")
 
-    def class_lists(n, src, R):
-        cp(n, T.NBU[:], src, R, ["NBU"])
-        ts(128, T.PHI[:], T.NBU[:], 128.0625, -15.0 / 32, mul, add, ["NBU"], ["PHI"])
-        ts(128, T.PHA[:], T.PHI[:], 2047, None, Op.bitwise_and, None, ["PHI"], ["PHA"])
-        cp(128, T.PHU[:], T.PHA[:], ["PHA"], ["PHU"])
-
-    def invert_piece(k, first):
-        win = T.W32[:, 0:2048].indirect(T.PHU[:, 16 * k:16 * k + 16])
-        src = T.IO[:, 256 * k:256 * k + 256]
-        op(CFG["inv"], lambda q: V.tensor_copy(win, src) if q == "v" else S.activation(win, src, Act.Silu), 256 * SC,
-           ["PHU", "IO.%d" % (k // 2)], ["W32"], table=first)
-
-    def invert(t):
-        for k in range(8):
-            invert_piece(k, t == 0 and k == 0)
+    def invert(off):
+        w = CFG["inv"]
+        for k in range(0, 8, w):
+            def piece(q, k=k):
+                win = T.W32[:, 0:2048].indirect(off[0][:, off[1] + 16 * k:off[1] + 16 * (k + w)])
+                src = T.IO[:, 256 * k:256 * (k + w)]
+                return V.tensor_copy(win, src) if q == "v" else S.activation(win, src, Act.Silu)
+            op("vs", piece, ("s", 256 * w), [off[2], "table"] + parts("IO")[k:k + w], ["W32"])
         dma("y", T.IVF[:], T.W32[0:128:16, :], 65536, ["W32"], ["IVF"])
         ts(128, T.IV[:], T.IVF[:], -64.0, None, add, None, ["IVF"], ["IV"])
 
-    def sites_in_class_order():
-        gather("A", "X", "NBU")
+    def sites_in_class_order(off):
+        gather("A", "X", off)
         for c in range(4):
             a = T.A[:, 512 * c:512 * c + 512]
             R = parts("A")[2 * c:2 * c + 2]
@@ -318,60 +398,64 @@ def rank_program(g, core, T, topo):
             scan(256, T.MN[:, 512 * c:512 * c + 512], T.BIG[:], a, add, mn, R + ["BIG"], ["MN.%d" % c])
 
     def hashes(n, plus, minus, R, x):
-        items = []
-        for k, (wp, wn) in enumerate((("W1", "W1N"), ("W2", "W2N"))):
-            out = T.PU[:, k * n:k * n + n]
-            items.append((out, T[wp][:], plus, True, minus is None))
-            if minus is not None:
-                items.append((out, T[wn][:], minus, False, True))
-        items.append((T.PU[0:n, 256:384], plus, T.IBN[:], True, minus is None))
+        UQ, UR, PP, HI, HU, HF, SN = [nm + x for nm in ("UQ", "UR", "PP", "HI", "HU", "HF", "SN")]
+        mms(2 * n, [(T.PA[:, 0:2 * n], T.CA[0:2, :], T.ZO[0:2, 0:2 * n], True, False)], ["CA", "ones"], "PA")
+        mms(2 * n, [(T.PB[:, 0:2 * n], T.CM[0:1, :], T.ZO[0:1, 256 - n:256 + n], True, False)], ["CM", "ones", "zeros"], "PB")
+        for bk in ("PA", "PB"):
+            items = []
+            for k in range(2):
+                out = T[bk][:, k * n:k * n + n]
+                items.append((out, T.W[:, 128 * k:128 * k + 128], plus, False, minus is None and k == 1))
+                if minus is not None:
+                    items.append((out, T.WN[:, 128 * k:128 * k + 128], minus, False, k == 1))
+            mms(max(n, 64) * len(items), items, R + ["W0", "W1", "WN"], bk)
+        ts(2 * n, T[UQ][:, 0:2 * n], T.PA[:, 0:2 * n], ROUND, ROUND, add, sub, [], [UQ], ["PA"])
+        items = [(T.PA[0:n, 256:384], plus, T.IBN[:], True, minus is None)]
         if minus is not None:
-            items.append((T.PU[0:n, 256:384], minus, T.IB[:], False, True))
-        mms(128 * len(items), items, R + ["W1", "W2", "W1N", "W2N", "IB", "IBN"], "PU")
-        UI, UA, U1, PP, HI, HU, SN = [nm + x for nm in ("UI", "UA", "U1", "PP", "HI", "HU", "SN")]
-        cp(2 * n, T[UI][:, 0:2 * n], T.PU[:, 0:2 * n], [], [UI], ["PU"])
-        op("vs", lambda q: copy(q, T[SN][0:n, :], T.PU[0:n, 256:384]), 128, [], [SN], ["PU"])
-        ts(2 * n, T[UA][:, 0:2 * n], T[UI][:, 0:2 * n], 2047, None, Op.bitwise_and, None, [UI], [UA])
-        ts(n, T[U1][:, 0:n], T[UA][:, 0:n], cM, None, add, None, [UA, "cM"], [U1])
-        tt(2 * n, T[PP][:, 0:n], T[U1][:, 0:n], T[UA][:, n:2 * n], mul, [U1, UA], [PP])
+            items.append((T.PA[0:n, 256:384], minus, T.IB[:], False, True))
+        mms(128 * len(items), items, R + ["IB", "IBN"], "PA")
+        op("vs", lambda q: copy(q, T[SN][0:n, :], T.PA[0:n, 256:384]), 128, [], [SN], ["PA"])
+        tt(2 * n, T[UR][:, 0:2 * n], T.PB[:, 0:2 * n], T[UQ][:, 0:2 * n], sub, [UQ], [UR], ["PB"])
+        tt(2 * n, T[PP][:, 0:n], T[UR][:, 0:n], T[UR][:, n:2 * n], mul, [UR], [PP])
         ts(n, T[HI][:, 0:n], T[PP][:, 0:n], 5, 2047, Op.arith_shift_right, Op.bitwise_and, [PP], [HI])
         cp(n, T[HU][:, 0:n], T[HI][:, 0:n], [HI], [HU])
+        ts(n, T[HF][:, 0:n], T[HI][:, 0:n], -2048.0, None, add, None, [HI], [HF])
+        K = "PK" + x
+        mms(2 * KW, [(T[K][0:n, KW:2 * KW], T[HF][:, 0:n], SPR, True, False),
+                     (T[K][0:n, KW:2 * KW], T[HF][:, 0:n], T.LMN[:, 241:241 + KW], False, True)], [HF, "SPR", "LMN"], K)
 
-    def events_by_centre(n, HI):
-        ts(n, T.HF[:, 0:n], T[HI][:, 0:n], -2048.0, 1.0 / 4096, add, mul, [HI], ["HF"])
-        mms(264, [(T.PH[0:n, 0:264], T.HF[:, 0:n], T.SPR[:], True, True)], ["HF", "SPR"], "PH")
-
-    def distances(n, lo, hi, bk, x, qs):
+    def distances(lo, hi, bk, x):
         w = 16 * (hi - lo)
-        mms(w, [(T[bk][:, 0:w], T["SN" + x][0:n, :], T.E[0:n, 16 * lo:16 * hi], True, False)], ["SN" + x, "E"], bk)
+        mms(w, [(T[bk][:, 0:w], T["SN" + x][lo:hi, :], T.E[lo:hi, 0:w], True, False)], ["SN" + x, "E"], bk)
         st = min(CFG["tp"], hi - lo)
         for a in range(lo, hi, st):
-            pick(16 * st, T.D[:, 16 * a:16 * (a + st)], T.TG[:, 0:2112].indirect(T["HU" + x][:, a:a + st]), TG + ["HU" + x],
-                 parts("D")[a // 16:(a + st) // 16], qs)
+            pick(16 * st, T.D[:, 16 * a:16 * (a + st)], T.TG[:, 0:2048].indirect(T["HU" + x][:, a:a + st]), ["TG", "HU" + x],
+                 parts("D")[a // 16:(a + st) // 16])
         mms(w, [(T[bk][:, 0:w], T.IB[:], T.D[:, 16 * lo:16 * hi], False, True)], ["IB"] + parts("D")[lo // 16:hi // 16], bk)
         op("s", lambda q: S.activation(T.R[:, 16 * lo:16 * hi], T[bk][:, 0:w], Act.Abs), w, [], ["R.%d" % (lo // 32)], [bk])
 
     def cost(lo, hi, K):
         R = ["R.%d" % c for c in range(lo // 32, (hi + 31) // 32)]
-        mms(16 * (hi - lo), [(T[K][lo:hi, m:264:33], T.R[:, 16 * lo + m:16 * hi:16], T.B1[:], True, True) for m in range(16)],
+        mms(16 * (hi - lo), [(T[K][lo:hi, 1 + m:KW:SG_W], T.R[:, 16 * lo + m:16 * hi:16], T.B1[:], True, True) for m in range(16)],
             R + ["B1"], K)
 
     def best_event(n, x):
         na = n // 16
-        K, KS, EQ, HS, Z, OE = [nm + x for nm in ("PK", "KS", "EQ", "HS", "Z3", "OE")]
-        scan(264, T[KS][0:n, :], T.C1[0:n, :], T[K][0:n, 0:264], add, mn, ["C1"], [KS], [K])
-        tt(247, T[EQ][0:n, 0:247], T[K][0:n, 0:247], T[KS][0:n, 17:264], Op.is_equal, [KS], [EQ], [K])
-        tt(247, T[HS][0:n, 0:247], T.PH[0:n, 0:247], T[EQ][0:n, 0:247], mul, [EQ], [HS], ["PH"])
-        scan(256, T[Z][0:n, 0:256], T.C2[0:n, 0:256], T[HS][0:n, 0:256], mul, add, ["C2", HS], [Z])
+        K, KS, NE, Z, OE = [nm + x for nm in ("PK", "KS", "NE", "Z", "OE")]
+        scan(KW, T[KS][0:n, :], T.C1[0:n, :], T[K][0:n, 0:KW], add, mn, ["C1"], [KS], [K])
+        tt(KW, T[NE][0:n, 1:KW], T[K][0:n, 1:KW], T[KS][0:n, 0:KW - 1], Op.is_ge, [KS], [NE], [K])
+        scan(KW, T[Z][0:n, 1:KW], T[NE][0:n, 1:KW], T[K][0:n, KW + 1:2 * KW], mul, add, [NE], [Z], [K])
         items = []
+        PO = T[K][:, 2 * KW:2 * KW + na]
         for gg in range(8):
-            w = slice(112 - 16 * gg, 240 - 16 * gg)
-            items.append((T.PO[:, 0:na], T.LMP[0:n, w], T[Z][0:n, 33 * gg + 16:33 * gg + 16 + na], gg == 0, False))
-            items.append((T.PO[:, 0:na], T.LMN[0:n, w], T[Z][0:n, 33 * gg + 17:33 * gg + 17 + na], False, gg == 7))
-        mms(1024, items, ["LMP", "LMN", Z], "PO")
-        ts(1, T[OE][:, 0:na], T.PO[:, 0:na], 4096.0, 2048.0, mul, add, [], [OE], ["PO"])
+            w, c = slice(112 - 16 * gg, 240 - 16 * gg), SG_W * gg + 17
+            items.append((PO, T.LM[0:n, w], T[Z][0:n, c:c + na], gg == 0, False))
+            items.append((PO, T.LMN[0:n, w], T[Z][0:n, c + 1:c + 1 + na], False, gg == 7))
+        mms(1024, items, ["LMP", "LMN", Z], K)
+        ts(1, T[OE][:, 0:na], PO, 2048.0, None, add, None, [], [OE], [K])
+        return PO
 
-    PS = T.PM[:, 256:257]
+    PS = T.PB[:, 480:481]
 
     def own_lookup(t):
         learn = t < ST - 1
@@ -379,74 +463,79 @@ def rank_program(g, core, T, topo):
         hashes(128, top, low, ends, "")
         if learn:
             tt(256, T.SG[:, 0:128], top, low, sub, ends, ["SG"])
-        events_by_centre(128, "HI")
-        if t == 0:
-            mms(256, [(T.PK[:, 17:264:33], T.ONE[:, 0:128], T.TH8[:], True, True)], ["ONE", "TH8"], "PK")
-        for c, bk in enumerate(("PD0", "PD1", "PM", "PU")):
-            distances(128, 32 * c, 32 * c + 32, bk, "", CFG["tags"][c])
+        for c in range(4):
+            distances(32 * c, 32 * c + 32, "PD%d" % c, "")
             cost(32 * c, 32 * c + 32, "PK")
         if t > 0:
             ow, rb = "OW%d" % (t - 1), "RB%d" % (t - 1)
-            cp(48 * SC, T.EF[:, 0:2112].indirect(T[ow][:, 0:3]), T[rb][:], [ow, rb], EF)
-        best_event(128, "")
+            cp(("s", 48), T.EF[:, 0:2112].indirect(T[ow][:, 0:3]), T[rb][:], [ow, rb], EF)
+        PO = best_event(128, "")
         if learn:
-            ts(1, T.OF[:], T.PO[:, 0:8], -1.0 / 8192, None, Op.is_gt, None, [], ["OF"], ["PO"])
-        tt(128 * GA, T.VE[:], T.EF[:, 0:2112].indirect(T.OE[:]), T.BASE[:], add, EF + ["OE", "BASE"], ["VE"])
+            ts(1, T.OF[:], PO, -0.5, None, Op.is_gt, None, [], ["OF"], ["PK"])
+        tt(("g", 128), T.VE[:], T.EF[:, 0:2049].indirect(T.OE[:]), T.BASE[:], add, EF + ["OE", "BASE"], ["VE"])
         ts(128, T.OS[:], T.VE[:], 1.0 / 16, -15.0 / 32, mul, add, ["VE"], ["OS"])
 
-    def next_class():
-        ts(1, T.CC[:], T.KS[:, 16::33], MAGIC, MAGIC, add, sub, ["KS"], ["CC"])
-        op("v", lambda q: V.tensor_reduce(T.RC[:, 0:1], T.CC[:], AxisListType.X, add), 1, ["CC"], ["RC"])
-        mms(256, [(PS, T.ONE[:, 0:128], T.RC[:, 0:1], True, True)], ["ONE", "RC"], "PM")
-        ts(1, T.QI[:, 0:1], PS, 1.0 / 16, -15.0 / 32, mul, add, [], ["QI"], ["PM"])
-        ts(1, T.NC[:, 0:1], T.QI[:, 0:1], 16.0, PS, mul, sub, ["QI"], ["NC"], ["PM"])
+    def next_class(turns, name):
+        least = T.KS[:, 16::SG_W]
+        op("vs", lambda q: V.tensor_reduce(T.RC[:, 0:1], least, AxisListType.X, add) if q == "v"
+           else S.activation(T.CC[:], least, Act.Identity, accum_out=T.RC[:, 0:1]), 1, ["KS"], ["RC", "CC"])
+        mms(256, [(PS, T.ONE[:], T.RC[:, 0:1], True, True)], ["ONE", "RC"], "PB")
+        ts(1, T.QI[:, 0:1], PS, 1.0 / 16, -15.0 / 32, mul, add, [], ["QI"], ["PB"])
+        ts(1, T.NC[:, 0:1], T.QI[:, 0:1], 16.0, PS, mul, sub, ["QI"], ["NC"], ["PB"])
         ts(1, T.OC[:], T.I8S[:], T.NC[:, 0:1], 128.0, sub, mul, ["I8S", "NC"], ["OC"])
-        class_lists(128 * GA, T.NB[:, 0:2048].indirect(T.OC[:]), ["NB", "OC"])
+        w = 128 * len(turns)
+        for k, s in enumerate(turns):
+            low = 2.0 ** (s - 11)
+            ts(("g", 128), T.PHI[:, 128 * k:128 * k + 128], T.NB[:, 0:2048].indirect(T.OC[:]), 2.0 ** s + low, (low - 1) / 2, mul, add,
+               ["NB", "OC"], ["PHI%d" % k])
+        ts(w, T.PHA[:, 0:w], T.PHI[:, 0:w], 2047, None, Op.bitwise_and, None, ["PHI0", "PHI1"], ["PHA"])
+        cp(w, T[name][:], T.PHA[:, 0:w], ["PHA"], [name])
 
     def ask(t):
         sc = "SC%d" % t
-        cp(128 * GA, T.FL[:], T.J[:, 0:8].indirect(T.OF[:]), ["J", "OF"], ["FL"])
-        scan(64, T.CN[:], T.RS[:, 0:128], T.FL[:], mul, add, ["RS", "FL"], ["CN"])
+        cp(("g", 128), T.FL[:], T.J[:, 0:8].indirect(T.OF[:]), ["J", "OF"], ["FL"])
+        scan(64, T.CN[:], T.ZO[:, 0:128], T.FL[:], mul, add, ["ones", "FL"], ["CN"])
         for a in range(3):
             ts(64, T.LE[:, 128 * a:128 * a + 128], T.CN[:], T.I8[:, a:a + 1], None, Op.is_le, None, ["CN", "I8"], ["LE%d" % a])
         scan(192, T.LS[:], T.RS[:], T.LE[:], mul, add, ["RS", "LE0", "LE1", "LE2"], ["LS"])
         cp(1, T.L1[:, 0:3], T.LS[:, 127::128], ["LS"], ["L1"])
-        cp(48 * GA, T[sc][:], T.SG[:, 0:144].indirect(T.L1[:, 0:3]), ["SG", "SGb", "L1"], [sc])
+        pick(48, T[sc][:], T.SG[:, 0:144].indirect(T.L1[:, 0:3]), ["SG", "SGb", "L1"], [sc])
         send((rank + 1 + t) % N, "RQ%d" % t, sc, "rq%d" % t, "sq%d" % t)
 
     def writers(t):
-        ts(48 * GA, T.HC[:], T.HI[:, 0:136].indirect(T.L1[:, 0:3]), -2048.0, 1.0 / 4096, add, mul, ["HI", "HIb", "L1"], ["HC"])
+        ts(("g", 48), T.HC[:], T.HI[:, 0:136].indirect(T.L1[:, 0:3]), -2048.0, 1.0 / 4096, add, mul, ["HI", "HIb", "L1"], ["HC"])
         items = []
         for a in range(3):
-            out = T.PM[:, 49 * a + 1:49 * a + 49]
+            out = T.PB[:, 256 + 49 * a + 1:256 + 49 * a + 49]
             items.append((out, T.P0[:], T.HC[:], True, False))
-            items.append((out, T.IB[:], T.MASK[:, 48 * a:48 * a + 48], False, True))
+            items.append((out, T.L16[0:16, :], T.MK[0:16, 48 * a:48 * a + 48], False, True))
         for b in range(16):
-            items.append((T.PM[:, 200:203], T.SEL[:, 15 - b:143 - b], T.HC[:, b:48:16], b == 0, b == 15))
-        mms(64 * 22, items, ["P0", "HC", "IB", "SEL", "MASK0", "MASK1", "MASK2"], "PM")
+            items.append((T.PB[:, 440:443], T.SEL[:, 15 - b:143 - b], T.HC[:, b:48:16], b == 0, b == 15))
+        mms(64 * 22, items, ["P0", "HC", "SEL", "L16", "MK"], "PB")
         for a in range(3):
-            col = T.PM[:, 200 + a:201 + a]
-            ts(48, T.VAL[:, 49 * a + 1:49 * a + 49], T.PM[:, 49 * a + 1:49 * a + 49], col, col, Op.is_equal, add, [], ["VAL%d" % a], ["PM"])
-        scan(147, T.YS[:, 0:147], T.VAL[:, 0:147], T.CAP[:, 0:147], mx, mn,
-             ["VALz", "VAL0", "VAL1", "VAL2", "CAP0", "CAP1", "CAP2"], ["YS"])
+            col = T.PB[:, 440 + a:441 + a]
+            ts(48, T.VAL[:, 49 * a + 1:49 * a + 49], T.PB[:, 256 + 49 * a + 1:256 + 49 * a + 49], col, col, Op.is_equal, add,
+               [], ["VAL%d" % a], ["PB"])
+        scan(147, T.YS[:, 0:147], T.VAL[:, 0:147], T.CAP[:, 0:147], mx, mn, ["VALz", "VAL0", "VAL1", "VAL2", "CAP"], ["YS"])
         ts(1, T["OW%d" % t][:, 0:3], T.YS[:, 48:147:49], 4096.0, 2048.0, mul, add, ["YS"], ["OW%d" % t])
 
     def serve(t):
         rq, an = "RQ%d" % t, "AN%d" % t
         hashes(NQ, T[rq][:], None, [rq], "2")
-        events_by_centre(NQ, "HI2")
-        distances(NQ, 0, 32, "PD0", "2", CFG["far"][0])
-        distances(NQ, 32, 48, "PD1", "2", CFG["far"][1])
+        distances(0, 32, "PD0", "2")
+        distances(32, 48, "PD1", "2")
         cost(0, NQ, "PK2")
         best_event(NQ, "2")
-        ts(48 * GA, T.RI[:], T.EF[:, 0:2112].indirect(T.OE2[:, 0:3]), 16.0625, -15.0 / 32, mul, add, EF + ["OE2"], ["RI"])
+        ts(("g", 48), T.RI[:], T.EF[:, 0:2049].indirect(T.OE2[:, 0:3]), 16.0625, -15.0 / 32, mul, add, EF + ["OE2"], ["RI"])
         ts(48, T[an][:], T.RI[:], 255, None, Op.bitwise_and, None, ["RI"], [an])
         send((rank - 1 - t) % N, "RB%d" % t, an, "rb%d" % t, "sb%d" % t)
 
-    class_lists(128, T.NB0[:], ["NB0"])
+    cp(128, T.L0[:], T.NB0[:], ["NB0"], ["L0"])
+    lists = (("L0", 0), ("L1S", 0), ("L2", 128))
     for t in range(ST):
-        sites_in_class_order()
-        invert(t)
+        name, at = lists[t]
+        sites_in_class_order(name)
+        invert((T[name], at, name))
         own_lookup(t)
         gather("A2", "A", "OS")
         if t == ST - 1:
@@ -458,10 +547,10 @@ def rank_program(g, core, T, topo):
             break
         gather("X", "A2", "IV")
         ask(t)
-        next_class()
+        next_class(((4,), (8, 7))[t], lists[t + 1][0])
         writers(t)
         serve(t)
-        cp(48 * SC, T.TG[:, 0:2112].indirect(T["OW%d" % t][:, 0:3]), T["SC%d" % t][:], ["OW%d" % t, "SC%d" % t], TG)
+        cp(("s", 48), T.TG[:, 0:2112].indirect(T["OW%d" % t][:, 0:3]), T["SC%d" % t][:], ["OW%d" % t, "SC%d" % t], ["TG"])
 
     known = {q: {} for q in Q}
     total = {}
@@ -484,8 +573,10 @@ def rank_program(g, core, T, topo):
                 if known[q].get(k2, 0) < v2:
                     known[q][k2] = v2
 
+    if "order" not in MEMO:
+        MEMO["order"] = schedule(ops)
     ndma = 0
-    for k, q in schedule(ops):
+    for k, q in MEMO["order"]:
         o = ops[k]
         ev = [wrote[r] for r in o["R"] + o["W"] if r in wrote]
         for w in o["W"]:

from concourse.mybir import AluOpType, AxisListType, ActivationFunctionType

F, B, I, U, H = "float32", "bfloat16", "int32", "uint16", "float16"
SG_W = 26
KW = 8 * SG_W
SCRATCH = {}
for _n in ("X", "A", "A2", "MX", "MN", "D", "R"):
    SCRATCH[_n] = ("sbuf", [128, 2048], B)
for _n, _w, _d in (
        ("SG", 144, B), ("SN", 128, B), ("IB", 128, B), ("IBN", 128, B), ("E", 512, B),
        ("TG", 2112, B), ("EF", 2112, B), ("NB", 2048, I), ("NB0", 128, I), ("IO", 2048, F), ("W32", 2048, F),
        ("IVF", 128, F), ("IV", 128, U), ("PHI", 256, I), ("PHA", 256, I), ("L0", 128, U), ("L1S", 128, U), ("L2", 256, U),
        ("WW", 8, B), ("TH", 8, I), ("PI", 8, I), ("CI", 8, B), ("CF", 16, F), ("JE", 512, B),
        ("J", 240, B), ("LM", 456, H), ("LMN", 456, H), ("ZO", 512, B), ("CA", 128, B), ("CM", 128, B),
        ("RST", 512, B), ("BIG", 512, B), ("W", 256, B), ("WN", 256, B), ("B1", 8, B),
        ("TH8", 8, F), ("ONE", 128, F), ("KC", KW, B), ("C1", KW, B),
        ("KS", KW, F), ("NE", KW, B), ("Z", KW, H), ("KS2", KW, F), ("NE2", KW, B), ("Z2", KW, H),
        ("BASE", 128, F), ("I8", 8, F), ("I8S", 8, F), ("RS", 384, B), ("P0", 128, B), ("SEL", 144, B),
        ("L16", 128, B), ("MK", 144, B), ("CAP", 152, F), ("VAL", 152, F), ("YS", 152, F),
        ("UQ", 256, F), ("UR", 256, F), ("PP", 128, I), ("HI", 136, I), ("HU", 128, U), ("HF", 128, H),
        ("UQ2", 96, F), ("UR2", 96, F), ("PP2", 48, I), ("HI2", 48, I), ("HU2", 48, U), ("HF2", 48, H), ("SN2", 128, B),
        ("OE", 8, U), ("OF", 8, U), ("VE", 128, F), ("OS", 128, U), ("OE2", 8, U),
        ("CC", 8, F), ("RC", 8, F), ("QI", 8, I), ("NC", 8, F), ("OC", 8, U),
        ("FL", 128, B), ("CN", 128, B), ("LE", 384, B), ("LS", 384, B), ("L1", 8, U), ("HC", 48, H),
        ("OW0", 8, U), ("OW1", 8, U), ("SC0", 48, B), ("SC1", 48, B), ("RQ0", 48, B), ("RQ1", 48, B),
        ("RI", 48, I), ("AN0", 48, I), ("AN1", 48, I), ("RB0", 48, I), ("RB1", 48, I)):
    SCRATCH[_n] = ("sbuf", [128, _w], _d)
for _n in ("PK", "PK2", "PA", "PB", "PD0", "PD1", "PD2", "PD3"):
    SCRATCH[_n] = ("psum", [128, 512], F)

SEMAPHORES = ["cg", "cv", "cs", "ct", "rq0", "rq1", "rb0", "rb1", "sq0", "sq1", "sb0", "sb1"] + ["d%d" % _i for _i in range(24)]

ST, NQ = 3, 48
ROUND = 1.5 * 2.0 ** 34
HUGE = 2.0 ** 20
MODELS = (
    {"f": 1.08, "ga": 1.56, "sc": 3.6, "fix": 0.03, "wake": 0.1, "dma": 1.0, "bw": 350e3, "rem": 1.6, "first": 1.5},
    {"f": 1.0, "ga": 1.4, "sc": 2.8, "fix": 0.05, "wake": 0.2, "dma": 1.5, "bw": 300e3, "rem": 2.5, "first": 2.5},
    {"f": 1.4, "ga": 1.9, "sc": 5.0, "fix": 0.03, "wake": 0.1, "dma": 1.0, "bw": 350e3, "rem": 2.0, "first": 2.0},
)
CFG = {"piece": 2, "inv": 1, "tp": 16, "out": [4, 6, 8], "seed": 1, "tries": 150000, "tight": 0.1, "heat": 0.6}
CYC, PECYC = 0.83e-3, 0.417e-3
MEMO = {}


def schedule(ops):
    n = len(ops)
    pred = [set() for _ in ops]
    wrote, readers, bank = {}, {}, {}
    for k, o in enumerate(ops):
        for r in o["R"] + o["after"]:
            if r in wrote:
                pred[k].add(wrote[r])
        for w in o["W"]:
            if w in wrote:
                pred[k].add(wrote[w])
            pred[k].update(readers.get(w, []))
        for b in o["P"]:
            if b in bank:
                pred[k].add(bank[b])
            bank[b] = k
        for r in o["R"]:
            readers.setdefault(r, []).append(k)
        for w in o["W"] + o["marks"]:
            wrote[w] = k
            readers[w] = []
        pred[k].discard(k)
    pred = [sorted(p) for p in pred]
    succ = [[] for _ in ops]
    for k in range(n):
        for p in pred[k]:
            succ[p].append(k)

    def times(m):
        busy, late, sends = [], [], 0
        for o in ops:
            fix, plain, ga, sc = o["cost"]
            if o["kind"] == "c":
                busy.append(m["f"] * (fix + CYC * (plain + ga * m["ga"] + sc * m["sc"])) + (m["fix"] if plain and not fix else 0.0))
                late.append(0.0)
            elif o["kind"] == "d":
                busy.append(0.06)
                late.append(m["dma"] + plain / m["bw"])
            else:
                busy.append(0.5)
                late.append(m["rem"] + (0.0 if sends else m["first"]))
                sends += 1
        lag = [[late[p] + (0.0 if ops[p]["qs"] == ops[k]["qs"] == "t" else m["wake"]) for p in pred[k]] for k in range(n)]
        return busy, late, lag

    costs = [times(m) for m in MODELS]

    QI = {q: i for i, q in enumerate("gvsty")}
    rows = [[(p, costs[0][2][k][j], costs[1][2][k][j], costs[2][2][k][j]) for j, p in enumerate(pred[k])] for k in range(n)]
    dur = [(costs[0][0][k], costs[1][0][k], costs[2][0][k]) for k in range(n)]
    tail = [k for k in range(n) if not succ[k]]
    moved = [[ops[k]["cost"][1] / m["bw"] for m in MODELS] if ops[k]["kind"] == "d" else None for k in range(n)]
    wa, wb, wc = [1.0 / m["f"] for m in MODELS]

    def worth(order, where):
        fa, fb, fc = [0.0] * 5, [0.0] * 5, [0.0] * 5
        da, db, dc = [0.0] * n, [0.0] * n, [0.0] * n
        lane = [0.0] * 3
        for k in order:
            q = where[k]
            a, b, c = fa[q], fb[q], fc[q]
            for p, la, lb, lc in rows[k]:
                la += da[p]
                if la > a:
                    a = la
                lb += db[p]
                if lb > b:
                    b = lb
                lc += dc[p]
                if lc > c:
                    c = lc
            u = dur[k]
            fa[q] = da[k] = a + u[0]
            fb[q] = db[k] = b + u[1]
            fc[q] = dc[k] = c + u[2]
            if moved[k]:
                for i, (s, d) in enumerate(((a, da), (b, db), (c, dc))):
                    lane[i] = max(lane[i], s + MODELS[i]["dma"]) + moved[k][i]
                    d[k] = max(d[k], lane[i] - costs[i][1][k])
        end = sum(w * max(d[k] + c[1][k] for k in tail) for w, d, c in ((wa, da, costs[0]), (wb, db, costs[1]), (wc, dc, costs[2])))
        return end + CFG["tight"] * (sum(da) + sum(db)) / n

    def sweep(prio, bias):
        busy, late, lag = costs[0]
        left = [len(b) for b in pred]
        ready = [(prio[k], k) for k in range(n) if not left[k]]
        taken = {q: [] for q in "gvsty"}
        start, where = [0.0] * n, [""] * n
        while ready:
            e = min(ready)
            ready.remove(e)
            k = e[1]
            can, b = 0.0, busy[k]
            for p, g_ in zip(pred[k], lag[k]):
                if start[p] + busy[p] + g_ > can:
                    can = start[p] + busy[p] + g_
            best = None
            for q in ops[k]["qs"]:
                t, s = taken[q], can
                at = len(t)
                while at and t[at - 1][1] > can:
                    at -= 1
                while at < len(t) and s + b > t[at][0] + 1e-9:
                    s = max(s, t[at][1])
                    at += 1
                s_cmp = s + (bias[k] if q == "v" else 0.0)
                if best is None or s_cmp < best[0]:
                    best = (s_cmp, s, q, at)
            _, s, q, at = best
            taken[q].insert(at, (s, s + b))
            start[k], where[k] = s, q
            for y in succ[k]:
                left[y] -= 1
                if not left[y]:
                    ready.append((prio[y], y))
        order = [(k, where[k]) for k in sorted(range(n), key=lambda j: (start[j], j))]
        return order, start

    x = [12345 + 977 * CFG["seed"]]

    def rnd():
        x[0] = (x[0] * 1103515245 + 12345) % 2147483648
        return x[0] / 2147483648

    busy, late, lag = costs[0]
    prio = [0.0] * n
    for k in reversed(range(n)):
        prio[k] = min([prio[k], -late[k]]) - busy[k]
        for p, g_ in zip(pred[k], lag[k]):
            prio[p] = min(prio[p], prio[k] - g_)
    first, start = sweep(prio, [0.3] * n)
    order, where = [k for k, q in first], [0] * n
    for k, q in first:
        where[k] = QI[q]
    now = worth(order, where)
    best = (now, order, where)
    either = [k for k in range(n) if len(ops[k]["qs"]) > 1]
    tries = CFG["tries"]
    for it in range(tries):
        o2, w2 = order, where
        z = rnd()
        if z < 0.2:
            k = either[int(rnd() * len(either))]
            w2 = list(where)
            other = [QI[q] for q in ops[k]["qs"] if QI[q] != where[k]]
            w2[k] = other[int(rnd() * len(other))]
            i = order.index(k)
        else:
            i = int(rnd() * n)
            k = order[i]
        if z > 0.1:
            hops, step = 1 + int(5 * rnd() * rnd()), (-1 if rnd() < 0.5 else 1)
            j = i
            while hops and 0 <= j + step < n:
                j += step
                hops -= w2[order[j]] == w2[k]
            links = pred if step < 0 else succ
            span = order[j:i + 1][::-1] if step < 0 else order[i:j + 1]
            tied, go, stay = set(links[k]), [k], []
            for y in span[1:]:
                if y in tied:
                    go.append(y)
                    tied.update(links[y])
                else:
                    stay.append(y)
            if step < 0:
                o2 = order[:j] + go[::-1] + stay[::-1] + order[i + 1:]
            else:
                o2 = order[:i] + stay + go + order[j + 1:]
        w = worth(o2, w2)
        if w <= now + CFG["heat"] * (1.0 - it / tries) * rnd() ** 3:
            now, order, where = w, o2, w2
            if w < best[0]:
                best = (w, o2, w2)
    MEMO["worth"] = best[0]
    return [(k, "gvsty"[best[2][k]]) for k in best[1]]


def rank_program(g, core, T, topo):
    rank = T.rank_of(core)
    if rank is None:
        return
    N = len(T.cores)
    Op, Act = AluOpType, ActivationFunctionType
    add, sub, mul, mx, mn = Op.add, Op.subtract, Op.mult, Op.max, Op.min
    Q = {"g": g, "v": g.vector, "s": g.scalar, "t": g.tensor, "y": g.sync}
    V, S, PE = g.vector, g.scalar, g.tensor
    ops = []

    def record(kind, qs, fn, R, W, P, cost, after=(), marks=(), sem=None):
        ops.append(dict(kind=kind, qs=qs, fn=fn, R=list(R), W=list(W), P=list(P), cost=cost, after=list(after),
                        marks=list(marks), sem=sem))

    def cost_of(n):
        if isinstance(n, tuple):
            return (0.058 + (n[2] if len(n) > 2 else 0.0), 0, n[1] if n[0] == "g" else 0, n[1] if n[0] == "s" else 0)
        return (0.0, max(n, 64), 0, 0)

    def op(qs, fn, n, R, W, P=()):
        after = ["sent." + r for r in R if r[:2] in ("RQ", "RB")]
        record("c", qs, lambda q: [fn(q)], R, W, P, cost_of(n), after=after)

    def dma(q, out, in_, nbytes, R, W):
        record("d", q, lambda q: Q[q].dma_start(out, in_), R, W, (), (0, nbytes, 0, 0))

    def send(dst_rank, name, src, rsem, lsem):
        dst = T.cores[dst_rank]
        rid, pid, _ = topo.addr(dst)
        record("r", "g", lambda q: g.remote_dma(T[name][:], T[src][:], T.sem[rsem], T.sem[lsem], pid, rid, topo.mask(core, dst)),
               [src], [], (), (0, 0, 0, 0), marks=["sent." + name], sem=(lsem, len(topo.engines(core, dst))))

    def ts(n, out, in0, s1, s2, o0, o1, R, W, P=()):
        if o1 is None:
            op("v", lambda q: V.tensor_scalar(out, in0, s1, None, o0), n, R, W, P)
        else:
            op("v", lambda q: V.tensor_scalar(out, in0, s1, s2, o0, o1), n, R, W, P)

    def tt(n, out, a, b, o, R, W, P=()):
        op("v", lambda q: V.tensor_tensor(out, a, b, o), n, R, W, P)

    def cp(n, out, in_, R, W, P=()):
        op("v", lambda q: V.tensor_copy(out, in_), n, R, W, P)

    def scan(n, out, d0, d1, o0, o1, R, W, P=()):
        op("v", lambda q: V.tensor_tensor_scan(out, d0, d1, 0.0, o0, o1), n, R, W, P)

    def fill(n, ap, c, W, P=()):
        op("v", lambda q: V.memset(ap, c), n, [], W, P)

    def mms(n, items, R, bk):
        after = ["sent." + r for r in R if r[:2] == "RQ"]
        record("c", "t", lambda q: [PE.matmul(*it) for it in items], R, [], [bk], (n * PECYC, 0, 0, 0), after=after)

    def gp(fn, n, R, W):
        record("c", "g", lambda q: [fn()], R, W, (), (0.15, 2 * n, 0, 0))

    def iota(n, out, pat, base, cm, W, flt=True):
        if flt:
            gp(lambda: g.iota(out, pat, base, cm, allow_small_or_imprecise_dtypes=True), n, [], W)
        else:
            gp(lambda: g.iota(out, pat, base, cm), n, [], W)

    def asel(n, out, in_, pat, cmp, base, cm, R, W, other=0.0):
        gp(lambda: g.affine_select(out, in_, pat, cmp, other, base, cm), n, R, W)

    def parts(name, n=8):
        return ["%s.%d" % (name, k) for k in range(n)]

    def copy(q, out, in_):
        return V.tensor_copy(out, in_) if q == "v" else S.activation(out, in_, Act.Copy)

    def pick(n, out, win, R, W, qs="vs"):
        op(qs, lambda q: copy(q, out, win), ("g", n), R, W)

    def gather(dst, src, off, k0=0, k1=8):
        w = CFG["piece"]
        for k in range(k0, k1, w):
            pick(256 * w, T[dst][:, 256 * k:256 * (k + w)], T[src][:, 0:2048].indirect(T[off][:, 16 * k:16 * (k + w)]),
                 parts(src) + [off], parts(dst)[k:k + w])

    cR, cG, c32, cP = [T.CI[:, k:k + 1] for k in range(4)]
    cT, cK = T.CF[:, 0:1], T.CF[:, 1:2]
    ones, zeros = T.ZO[:, 0:256], T.ZO[:, 256:512]
    JG = T.JE[:, 0:128]
    LMP, SPR = T.LM[:, 0:240], T.LM[:, 240:240 + KW]

    c0 = rank % 16
    dma("s", T.NB0[:], T.nb[:, 128 * c0:128 * c0 + 128], 65536, [], ["NB0"])
    dma("y", T.X[:], T.x[:], 524288, [], parts("X"))
    dma("y", T.WW[:, 0:2], T.w[:], 8192, [], ["WW"])
    dma("y", T.TG[:, 0:2048], T.tag[:], 524288, ["X.0"], ["TG"])
    dma("y", T.TH[:, 0:1], T.th[:], 8192, ["X.0"], ["TH"])
    dma("y", T.EF[:, 0:2048], T.ef[:], 524288, ["TG"], ["EFa"])
    dma("y", T.NB[:], T.nb[:], 1048576, ["EFa"], ["NB"])
    EF = ["EFa", "EFb"]

    fill(128, ones, 1.0, ["ones"])
    fill(128, zeros, 0.0, ["zeros"])
    iota(1, T.PI[:, 3:4], [[0, 1]], 0, 1, ["PI3"], False)
    iota(256, T.IO[:, 0:256], [[1, 256]], 64, 0, ["IO.0"])
    op("s", lambda q: S.activation(T.IO[:, 256:512], T.IO[:, 0:256], Act.Silu, 256.0), 256 + 1500, ["IO.0"], ["IO.1", "table"])
    for c in range(1, 4):
        iota(512, T.IO[:, 512 * c:512 * c + 512], [[1, 512]], 64 + 512 * c, 0, parts("IO")[2 * c:2 * c + 2])
    iota(128, JG, [[1, 8], [0, 16]], 0, 0, ["JG"])
    iota(384, T.JE[:, 128:512], [[1, 24], [0, 16]], 8, 0, ["JE"])
    asel(128, T.IB[:], T.ZO[:, 256:384], [[-1, 128]], Op.not_equal, 0, 1, ["zeros"], ["IB"], 1.0)
    asel(128, T.IBN[:], T.ZO[:, 256:384], [[-1, 128]], Op.not_equal, 0, 1, ["zeros"], ["IBN"], -1.0)
    iota(128, T.CA[0:2, :], [[0, 128]], -1024, 0, ["CA"])
    asel(128, T.CA[0:2, :], T.CA[0:2, :], [[0, 128]], Op.is_equal, 0, 1, ["CA"], ["CA"], 0.5)
    iota(128, T.CM[0:1, :], [[0, 8], [64, 16]], 32, 0, ["CM"])
    iota(240, T.J[:], [[1, 240]], 0, 0, ["J"])
    asel(KW, T.KC[:], T.ZO[:, 0:KW], [[0, 8], [16, SG_W]], Op.is_ge, -273, -1, ["ones"], ["KC"], -HUGE)
    asel(KW, T.C1[:], T.ZO[:, 256:256 + KW], [[0, 8], [1, SG_W]], Op.not_equal, 0, 0, ["zeros"], ["C1"], HUGE)
    iota(128, T.BASE[:], [[256, 128]], 0, 0, ["BASE"])
    iota(128, T.ONE[:], [[0, 128]], 1, 0, ["ONE"])
    iota(384, T.RS[:], [[0, 384]], 1, 0, ["RS"])
    iota(3, T.RS[:, 0::128], [[0, 3]], 0, 0, ["RS"])
    iota(16, T.SG[:, 128:144], [[0, 16]], 0, 0, ["SGb"])
    iota(8, T.HI[:, 128:136], [[0, 8]], 6144, 0, ["HIb"], False)
    asel(128, T.P0[:], T.ZO[:, 0:128], [[-16, 8], [0, 16]], Op.is_equal, 0, 1, ["ones"], ["P0"])
    iota(144, T.SEL[:], [[0, 144]], 0, 0, ["SEL"])
    asel(8, T.SEL[:, 15:143:16], T.ZO[:, 0:8], [[-16, 8]], Op.is_equal, 0, 1, ["ones"], ["SEL"])
    asel(128, T.L16[0:16, :], T.ZO[0:16, 0:128], [[0, 8], [-1, 16]], Op.is_equal, 0, 1, ["ones"], ["L16"])
    asel(144, T.MK[0:16, :], T.ZO[0:16, 0:144], [[-16, 3], [1, 48]], Op.is_ge, 0, -1, ["ones"], ["MK"])
    iota(3, T.VAL[:, 0:147:49], [[0, 3]], 0, 0, ["VALz"])
    iota(147, T.CAP[:, 0:147], [[0, 147]], 4, 0, ["CAP"])
    iota(3, T.CAP[:, 0:147:49], [[0, 3]], -1, 0, ["CAP"])

    fill(256, T.RST[:], 1.0, ["RST"])
    fill(256, T.BIG[:], 0.0, ["BIG"])
    fill(1, T.RST[:, 0::16], 0.0, ["RST"])
    fill(1, T.BIG[:, 0::16], 256.0, ["BIG"])
    ts(1, T.PI[:, 0:1], T.PI[:, 3:4], 15, None, Op.bitwise_and, None, ["PI3"], ["PI0"])
    ts(1, T.PI[:, 1:2], T.PI[:, 3:4], 4, None, Op.arith_shift_right, None, ["PI3"], ["PI1"])
    ts(1, T.PI[:, 2:3], T.PI[:, 3:4], 31, None, Op.bitwise_and, None, ["PI3"], ["PI2"])
    cp(1, T.CI[:, 0:4], T.PI[:, 0:4], ["PI0", "PI1", "PI2", "PI3"], ["cR"])
    for k in range(2):
        ts(64, T.W[:, 128 * k:128 * k + 128], JG, cG, T.WW[:, k:k + 1], Op.is_equal, mul, ["JG", "cR", "WW"], ["W%d" % k])
    ts(128, T.WN[:], T.W[:], -1.0, None, mul, None, ["W0", "W1"], ["WN"])
    ts(1, T.B1[:], T.JE[:, 0:128:16], cG, None, Op.is_equal, None, ["JG", "cR"], ["B1"])
    ts(256, T.E[:], T.JE[:], c32, None, Op.is_equal, None, ["JG", "JE", "cR"], ["E"])
    ts(1, cT, T.TH[:, 0:1], 0.5, 1.0 / 16, add, mul, ["TH"], ["cT"])
    ts(1, T.TH8[:], T.B1[:], cT, None, mul, None, ["B1", "cT"], ["TH8"])
    ts(1, cK, cG, 10.0, cP, mul, add, ["cR"], ["cK"])
    ts(120, LMP, T.J[:], cR, 112.0, sub, Op.is_equal, ["J", "cR"], ["LMP"])
    ts(108, T.LM[:, 240:456], T.J[:, 0:216], cK, 1.0, sub, Op.is_equal, ["J", "cK"], ["SPR"])
    ts(228, T.LMN[:], T.LM[:], -1.0, None, mul, None, ["LMP", "SPR"], ["LMN"])
    ts(1, T.EF[:, 2048:2049], cR, 17.0, None, mul, None, ["cR"], ["EFb"])
    ts(1, T.I8[:], T.JE[:, 0:128:16], 16.0, cR, mul, add, ["JG", "cR"], ["I8"])
    ts(1, T.I8S[:], T.I8[:], 1.0 / 128, None, mul, None, ["I8"], ["I8S"])
    ts(1, T.CAP[:, 48:147:49], T.I8[:, 0:3], 16.0, 1.0 / 4096, add, mul, ["I8"], ["CAP"])
    for K in ("PK", "PK2"):
        mms(KW, [(T[K][:, 0:KW], T.IBN[:], T.KC[:], True, True)], ["IBN", "KC"], K)
    mms(256, [(T.PK[:, 17:KW:SG_W], T.ONE[:], T.TH8[:], True, True)], ["ONE", "TH8"], "PK")

    def invert(off):
        w = CFG["inv"]
        for k in range(0, 8, w):
            def piece(q, k=k):
                win = T.W32[:, 0:2048].indirect(off[0][:, off[1] + 16 * k:off[1] + 16 * (k + w)])
                src = T.IO[:, 256 * k:256 * (k + w)]
                return V.tensor_copy(win, src) if q == "v" else S.activation(win, src, Act.Silu)
            op("vs", piece, ("s", 256 * w), [off[2], "table"] + parts("IO")[k:k + w], ["W32"])
        dma("y", T.IVF[:], T.W32[0:128:16, :], 65536, ["W32"], ["IVF"])
        ts(128, T.IV[:], T.IVF[:], -64.0, None, add, None, ["IVF"], ["IV"])

    def sites_in_class_order(off):
        gather("A", "X", off)
        for c in range(4):
            a = T.A[:, 512 * c:512 * c + 512]
            R = parts("A")[2 * c:2 * c + 2]
            scan(256, T.MX[:, 512 * c:512 * c + 512], T.RST[:], a, mul, mx, R + ["RST"], ["MX.%d" % c])
            scan(256, T.MN[:, 512 * c:512 * c + 512], T.BIG[:], a, add, mn, R + ["BIG"], ["MN.%d" % c])

    def hashes(n, plus, minus, R, x):
        UQ, UR, PP, HI, HU, HF, SN = [nm + x for nm in ("UQ", "UR", "PP", "HI", "HU", "HF", "SN")]
        mms(2 * n, [(T.PA[:, 0:2 * n], T.CA[0:2, :], T.ZO[0:2, 0:2 * n], True, False)], ["CA", "ones"], "PA")
        mms(2 * n, [(T.PB[:, 0:2 * n], T.CM[0:1, :], T.ZO[0:1, 256 - n:256 + n], True, False)], ["CM", "ones", "zeros"], "PB")
        for bk in ("PA", "PB"):
            items = []
            for k in range(2):
                out = T[bk][:, k * n:k * n + n]
                items.append((out, T.W[:, 128 * k:128 * k + 128], plus, False, minus is None and k == 1))
                if minus is not None:
                    items.append((out, T.WN[:, 128 * k:128 * k + 128], minus, False, k == 1))
            mms(max(n, 64) * len(items), items, R + ["W0", "W1", "WN"], bk)
        ts(2 * n, T[UQ][:, 0:2 * n], T.PA[:, 0:2 * n], ROUND, ROUND, add, sub, [], [UQ], ["PA"])
        items = [(T.PA[0:n, 256:384], plus, T.IBN[:], True, minus is None)]
        if minus is not None:
            items.append((T.PA[0:n, 256:384], minus, T.IB[:], False, True))
        mms(128 * len(items), items, R + ["IB", "IBN"], "PA")
        op("vs", lambda q: copy(q, T[SN][0:n, :], T.PA[0:n, 256:384]), 128, [], [SN], ["PA"])
        tt(2 * n, T[UR][:, 0:2 * n], T.PB[:, 0:2 * n], T[UQ][:, 0:2 * n], sub, [UQ], [UR], ["PB"])
        tt(2 * n, T[PP][:, 0:n], T[UR][:, 0:n], T[UR][:, n:2 * n], mul, [UR], [PP])
        ts(n, T[HI][:, 0:n], T[PP][:, 0:n], 5, 2047, Op.arith_shift_right, Op.bitwise_and, [PP], [HI])
        cp(n, T[HU][:, 0:n], T[HI][:, 0:n], [HI], [HU])
        ts(n, T[HF][:, 0:n], T[HI][:, 0:n], -2048.0, None, add, None, [HI], [HF])
        K = "PK" + x
        mms(2 * KW, [(T[K][0:n, KW:2 * KW], T[HF][:, 0:n], SPR, True, False),
                     (T[K][0:n, KW:2 * KW], T[HF][:, 0:n], T.LMN[:, 241:241 + KW], False, True)], [HF, "SPR", "LMN"], K)

    def distances(lo, hi, bk, x):
        w = 16 * (hi - lo)
        mms(w, [(T[bk][:, 0:w], T["SN" + x][lo:hi, :], T.E[lo:hi, 0:w], True, False)], ["SN" + x, "E"], bk)
        st = min(CFG["tp"], hi - lo)
        for a in range(lo, hi, st):
            pick(16 * st, T.D[:, 16 * a:16 * (a + st)], T.TG[:, 0:2048].indirect(T["HU" + x][:, a:a + st]), ["TG", "HU" + x],
                 parts("D")[a // 16:(a + st) // 16])
        mms(w, [(T[bk][:, 0:w], T.IB[:], T.D[:, 16 * lo:16 * hi], False, True)], ["IB"] + parts("D")[lo // 16:hi // 16], bk)
        op("s", lambda q: S.activation(T.R[:, 16 * lo:16 * hi], T[bk][:, 0:w], Act.Abs), w, [], ["R.%d" % (lo // 32)], [bk])

    def cost(lo, hi, K):
        R = ["R.%d" % c for c in range(lo // 32, (hi + 31) // 32)]
        mms(16 * (hi - lo), [(T[K][lo:hi, 1 + m:KW:SG_W], T.R[:, 16 * lo + m:16 * hi:16], T.B1[:], True, True) for m in range(16)],
            R + ["B1"], K)

    def best_event(n, x):
        na = n // 16
        K, KS, NE, Z, OE = [nm + x for nm in ("PK", "KS", "NE", "Z", "OE")]
        scan(KW, T[KS][0:n, :], T.C1[0:n, :], T[K][0:n, 0:KW], add, mn, ["C1"], [KS], [K])
        tt(KW, T[NE][0:n, 1:KW], T[K][0:n, 1:KW], T[KS][0:n, 0:KW - 1], Op.is_ge, [KS], [NE], [K])
        scan(KW, T[Z][0:n, 1:KW], T[NE][0:n, 1:KW], T[K][0:n, KW + 1:2 * KW], mul, add, [NE], [Z], [K])
        items = []
        PO = T[K][:, 2 * KW:2 * KW + na]
        for gg in range(8):
            w, c = slice(112 - 16 * gg, 240 - 16 * gg), SG_W * gg + 17
            items.append((PO, T.LM[0:n, w], T[Z][0:n, c:c + na], gg == 0, False))
            items.append((PO, T.LMN[0:n, w], T[Z][0:n, c + 1:c + 1 + na], False, gg == 7))
        mms(1024, items, ["LMP", "LMN", Z], K)
        ts(1, T[OE][:, 0:na], PO, 2048.0, None, add, None, [], [OE], [K])
        return PO

    PS = T.PB[:, 480:481]

    def own_lookup(t):
        learn = t < ST - 1
        top, low, ends = T.MX[:, 15::16], T.MN[:, 15::16], parts("MX", 4) + parts("MN", 4)
        hashes(128, top, low, ends, "")
        if learn:
            tt(256, T.SG[:, 0:128], top, low, sub, ends, ["SG"])
        for c in range(4):
            distances(32 * c, 32 * c + 32, "PD%d" % c, "")
            cost(32 * c, 32 * c + 32, "PK")
        if t > 0:
            ow, rb = "OW%d" % (t - 1), "RB%d" % (t - 1)
            cp(("s", 48), T.EF[:, 0:2112].indirect(T[ow][:, 0:3]), T[rb][:], [ow, rb], EF)
        PO = best_event(128, "")
        if learn:
            ts(1, T.OF[:], PO, -0.5, None, Op.is_gt, None, [], ["OF"], ["PK"])
        tt(("g", 128), T.VE[:], T.EF[:, 0:2049].indirect(T.OE[:]), T.BASE[:], add, EF + ["OE", "BASE"], ["VE"])
        ts(128, T.OS[:], T.VE[:], 1.0 / 16, -15.0 / 32, mul, add, ["VE"], ["OS"])

    def next_class(turns, name):
        least = T.KS[:, 16::SG_W]
        op("vs", lambda q: V.tensor_reduce(T.RC[:, 0:1], least, AxisListType.X, add) if q == "v"
           else S.activation(T.CC[:], least, Act.Identity, accum_out=T.RC[:, 0:1]), 1, ["KS"], ["RC", "CC"])
        mms(256, [(PS, T.ONE[:], T.RC[:, 0:1], True, True)], ["ONE", "RC"], "PB")
        ts(1, T.QI[:, 0:1], PS, 1.0 / 16, -15.0 / 32, mul, add, [], ["QI"], ["PB"])
        ts(1, T.NC[:, 0:1], T.QI[:, 0:1], 16.0, PS, mul, sub, ["QI"], ["NC"], ["PB"])
        ts(1, T.OC[:], T.I8S[:], T.NC[:, 0:1], 128.0, sub, mul, ["I8S", "NC"], ["OC"])
        w = 128 * len(turns)
        for k, s in enumerate(turns):
            low = 2.0 ** (s - 11)
            ts(("g", 128), T.PHI[:, 128 * k:128 * k + 128], T.NB[:, 0:2048].indirect(T.OC[:]), 2.0 ** s + low, (low - 1) / 2, mul, add,
               ["NB", "OC"], ["PHI%d" % k])
        ts(w, T.PHA[:, 0:w], T.PHI[:, 0:w], 2047, None, Op.bitwise_and, None, ["PHI0", "PHI1"], ["PHA"])
        cp(w, T[name][:], T.PHA[:, 0:w], ["PHA"], [name])

    def ask(t):
        sc = "SC%d" % t
        cp(("g", 128), T.FL[:], T.J[:, 0:8].indirect(T.OF[:]), ["J", "OF"], ["FL"])
        scan(64, T.CN[:], T.ZO[:, 0:128], T.FL[:], mul, add, ["ones", "FL"], ["CN"])
        for a in range(3):
            ts(64, T.LE[:, 128 * a:128 * a + 128], T.CN[:], T.I8[:, a:a + 1], None, Op.is_le, None, ["CN", "I8"], ["LE%d" % a])
        scan(192, T.LS[:], T.RS[:], T.LE[:], mul, add, ["RS", "LE0", "LE1", "LE2"], ["LS"])
        cp(1, T.L1[:, 0:3], T.LS[:, 127::128], ["LS"], ["L1"])
        pick(48, T[sc][:], T.SG[:, 0:144].indirect(T.L1[:, 0:3]), ["SG", "SGb", "L1"], [sc])
        send((rank + 1 + t) % N, "RQ%d" % t, sc, "rq%d" % t, "sq%d" % t)

    def writers(t):
        ts(("g", 48), T.HC[:], T.HI[:, 0:136].indirect(T.L1[:, 0:3]), -2048.0, 1.0 / 4096, add, mul, ["HI", "HIb", "L1"], ["HC"])
        items = []
        for a in range(3):
            out = T.PB[:, 256 + 49 * a + 1:256 + 49 * a + 49]
            items.append((out, T.P0[:], T.HC[:], True, False))
            items.append((out, T.L16[0:16, :], T.MK[0:16, 48 * a:48 * a + 48], False, True))
        for b in range(16):
            items.append((T.PB[:, 440:443], T.SEL[:, 15 - b:143 - b], T.HC[:, b:48:16], b == 0, b == 15))
        mms(64 * 22, items, ["P0", "HC", "SEL", "L16", "MK"], "PB")
        for a in range(3):
            col = T.PB[:, 440 + a:441 + a]
            ts(48, T.VAL[:, 49 * a + 1:49 * a + 49], T.PB[:, 256 + 49 * a + 1:256 + 49 * a + 49], col, col, Op.is_equal, add,
               [], ["VAL%d" % a], ["PB"])
        scan(147, T.YS[:, 0:147], T.VAL[:, 0:147], T.CAP[:, 0:147], mx, mn, ["VALz", "VAL0", "VAL1", "VAL2", "CAP"], ["YS"])
        ts(1, T["OW%d" % t][:, 0:3], T.YS[:, 48:147:49], 4096.0, 2048.0, mul, add, ["YS"], ["OW%d" % t])

    def serve(t):
        rq, an = "RQ%d" % t, "AN%d" % t
        hashes(NQ, T[rq][:], None, [rq], "2")
        distances(0, 32, "PD0", "2")
        distances(32, 48, "PD1", "2")
        cost(0, NQ, "PK2")
        best_event(NQ, "2")
        ts(("g", 48), T.RI[:], T.EF[:, 0:2049].indirect(T.OE2[:, 0:3]), 16.0625, -15.0 / 32, mul, add, EF + ["OE2"], ["RI"])
        ts(48, T[an][:], T.RI[:], 255, None, Op.bitwise_and, None, ["RI"], [an])
        send((rank - 1 - t) % N, "RB%d" % t, an, "rb%d" % t, "sb%d" % t)

    cp(128, T.L0[:], T.NB0[:], ["NB0"], ["L0"])
    lists = (("L0", 0), ("L1S", 0), ("L2", 128))
    for t in range(ST):
        name, at = lists[t]
        sites_in_class_order(name)
        invert((T[name], at, name))
        own_lookup(t)
        gather("A2", "A", "OS")
        if t == ST - 1:
            k0 = 0
            for k1 in CFG["out"]:
                gather("X", "A2", "IV", k0, k1)
                dma("y", T.y[:, 256 * k0:256 * k1], T.X[:, 256 * k0:256 * k1], 65536 * (k1 - k0), parts("X")[k0:k1], [])
                k0 = k1
            break
        gather("X", "A2", "IV")
        ask(t)
        next_class(((4,), (8, 7))[t], lists[t + 1][0])
        writers(t)
        serve(t)
        cp(("s", 48), T.TG[:, 0:2112].indirect(T["OW%d" % t][:, 0:3]), T["SC%d" % t][:], ["OW%d" % t, "SC%d" % t], ["TG"])

    known = {q: {} for q in Q}
    total = {}
    wrote, readers, bank = {}, {}, {}
    for t in range(ST - 1):
        for name, src, rsem in (("RQ%d" % t, (rank - 1 - t) % N, "rq%d" % t), ("RB%d" % t, (rank + 1 + t) % N, "rb%d" % t)):
            total[rsem] = len(topo.engines(T.cores[src], core))
            wrote[name] = (rsem, total[rsem], {})

    def need(q, events):
        best = {}
        for e in events:
            if e[0] not in best or best[e[0]][1] < e[1]:
                best[e[0]] = e
        for key, val, snap in sorted(best.values(), key=lambda e: -len(e[2])):
            if known[q].get(key, 0) < val:
                Q[q].wait_ge(T.sem[key], val)
                known[q][key] = val
            for k2, v2 in snap.items():
                if known[q].get(k2, 0) < v2:
                    known[q][k2] = v2

    if "order" not in MEMO:
        MEMO["order"] = schedule(ops)
    ndma = 0
    for k, q in MEMO["order"]:
        o = ops[k]
        ev = [wrote[r] for r in o["R"] + o["W"] if r in wrote]
        for w in o["W"]:
            ev.extend(readers.get(w, []))
        for b in o["P"]:
            ev.extend(e for q2, e in bank.get(b, {}).items() if q2 != q)
        need(q, ev)
        if o["kind"] == "c":
            key = "c" + q
            for ins in o["fn"](q):
                ins.then_inc(T.sem[key], 1)
                total[key] = total.get(key, 0) + 1
        elif o["kind"] == "d":
            key = "d%d" % ndma
            ndma += 1
            o["fn"](q).then_inc(T.sem[key], 16)
            total[key] = 16
        else:
            o["fn"](q)
            key = o["sem"][0]
            total[key] = o["sem"][1]
        e = (key, total[key], dict(known[q]))
        for r in o["R"]:
            readers.setdefault(r, []).append(e)
        for w in o["W"]:
            wrote[w] = e
            readers[w] = []
        for b in o["P"]:
            bank.setdefault(b, {})[q] = e
    need("y", [(key, val, {}) for key, val in sorted(total.items())])
